import numpy as np
import ml_dtypes


def mxq(x, axis, fmt="e4m3"):
    dtype, down = {"e4m3": (ml_dtypes.float8_e4m3fn, 7), "e5m2": (ml_dtypes.float8_e5m2, 14)}[fmt]
    v = np.moveaxis(np.asarray(x, np.float32).astype(ml_dtypes.bfloat16).astype(np.float64), axis, -1)
    blocks = v.reshape(v.shape[:-1] + (-1, 32))
    amax = np.abs(blocks).max(-1, keepdims=True)
    byte = np.maximum(np.where(amax > 0, np.frexp(amax)[1] - 1 + 127, 0) - down, 1)
    scale = np.exp2(byte - 127.0)
    codes = (blocks / scale).astype(np.float32).astype(dtype).astype(np.float64)
    return np.moveaxis((codes * scale).reshape(v.shape), -1, axis)


WIDE = False


def mx_kscale(k):
    if not WIDE:
        return np.ones(k)
    levels = np.array([10, -10, 5, -5, 0])
    if k % 512:
        return np.exp2(np.random.permutation(np.resize(levels, k // 32))).repeat(32)
    a = np.empty((k // 512, 16))
    for p in range(k // 512):
        a[p, :8] = np.random.permutation(np.resize(levels, 8))
        for g in range(8):
            far = levels[np.abs(levels - a[p, g]) >= 10]
            a[p, g + 8] = far[np.random.randint(len(far))]
    return np.exp2(a.ravel()).repeat(32)


def f64(x):
    return np.asarray(x).astype(np.float64)


def striped(idx):
    return np.tile(idx.reshape(-1, 16).T, (8, 1)).astype(np.uint16)


def unstriped(offs):
    return offs[:16].T.reshape(-1).astype(np.int64)


def pack_weight(w):
    k, n = w.shape
    w = f64(np.asarray(w, np.float32).astype(ml_dtypes.bfloat16)).reshape(k // 32, 32, n)
    amax = np.abs(w).max(1)
    byte = np.clip(np.where(amax > 0, np.frexp(amax)[1] - 1 + 127 - 7, 1), 1, 254)
    scaled = (w * np.exp2(127.0 - byte)[:, None, :]).reshape(k, n).astype(np.float32)
    words = np.ascontiguousarray(scaled.reshape(k // 512, 128, 4, n).transpose(0, 1, 3, 2)).astype(ml_dtypes.float8_e4m3fn).view(np.uint8)
    return words, np.ascontiguousarray(byte.astype(np.uint8).reshape(k // 512, 16, n))


def unpack_weight(words, scales):
    g, p, n, _ = words.shape
    vals = np.ascontiguousarray(words).view(ml_dtypes.float8_e4m3fn).astype(np.float64) * np.repeat(np.exp2(scales.astype(np.float64) - 127.0), 8, axis=1)[..., None]
    return vals.transpose(0, 1, 3, 2).reshape(g * 512, n)


def relu(v):
    return np.maximum(v, 0.0)


K, T, S, V, H, N, J = 1024, 2048, 1024, 512, 512, 128, 512


def setup_inputs():
    n = np.random.standard_normal
    s = mx_kscale(K)[:, None]
    u = mx_kscale(H)
    r = mx_kscale(J)[:, None]
    packed_xT = pack_weight(n((K, T)) * s)
    return {
        "x_words": packed_xT[0],
        "x_scales": packed_xT[1],
        "eT": (n((J, V)) * r).astype(np.float32),
        "w1": (n((K, H)) / np.sqrt(3 * K) / s * u).astype(np.float32),
        "w2": (n((K, H)) / np.sqrt(3 * K) / s * u).astype(np.float32),
        "w3": (n((J, H)) / np.sqrt(3 * J) / r * u).astype(np.float32),
        "w4": (n((H, N)) / np.sqrt(H) / u[:, None]).astype(np.float32),
        "offs": striped(np.random.permutation(T)[:S]),
    }


def reference(x_words, x_scales, eT, w1, w2, w3, w4, offs):
    xq = unpack_weight(x_words, x_scales)[:, unstriped(offs)]
    h = relu(mxq(f64(w1), 0, "e4m3").T @ xq[:, :V] + mxq(f64(w2), 0, "e4m3").T @ xq[:, V:2 * V] + mxq(f64(w3), 0, "e4m3").T @ mxq(f64(eT), 0, "e4m3"))
    return mxq(f64(w4), 0, "e4m3").T @ mxq(h, 0, "e4m3")

@@ -1,0 +1,171 @@
+from contextlib import ExitStack
+
+import concourse.mybir as mybir
+
+K, T, S, V, H, N, J = 1024, 2048, 1024, 512, 512, 128, 512
+FLOPS = 2 * (2 * K + J) * H * V + 2 * H * N * V
+
+F32 = mybir.dt.float32
+BF16 = mybir.dt.bfloat16
+I32 = mybir.dt.int32
+U32 = mybir.dt.uint32
+U16 = mybir.dt.uint16
+U8 = mybir.dt.uint8
+FP8X4 = mybir.dt.float8_e4m3fn_x4
+ACT = mybir.ActivationFunctionType
+
+P = 128
+PACK = 4
+K_PASS = P * PACK
+CHUNK = 128
+CHUNKS = V // CHUNK
+E_LOADS = [[0,1],[2,3]]
+VECTOR_SHARE = [0,0,48,80,88]
+E_CAST_ON_VECTOR = [1,0,1,0]
+RELU_ON_VECTOR = [0,0,1,0]
+OUT_ON_VECTOR = [1,1,0,1]
+
+
+def tile_picked_edgeup_relu_p_kernel(tc, x_words, x_scales, eT, w1, w2, w3, w4, offs, out):
+    nc = tc.nc
+    with ExitStack() as ctx:
+        sb = ctx.enter_context(tc.tile_pool(name="sb", bufs=1))
+        ps = ctx.enter_context(tc.psum_pool(name="ps", bufs=1))
+
+        def cast(on_vector, dst, src):
+            if on_vector:
+                nc.vector.tensor_copy(out=dst, in_=src)
+            else:
+                nc.scalar.activation(out=dst, in_=src, func=ACT.Copy)
+
+        def quantize(name, grouped, width):
+            codes = sb.tile([P, width], U32, name=name + "_codes", align_bytes=64)
+            scales = sb.tile([P, width], U8, name=name + "_scales", align_bytes=64)
+            nc.vector.quantize_mx(out=codes[:].bitcast(FP8X4), scales=scales[:], in_=grouped)
+            return codes, scales
+
+        offsets = sb.tile([P, S // 16], U16, name="offsets")
+        x_plane = sb.tile([P, T], U8, name="x_plane", align_bytes=64)
+        nc.gpsimd.memset(x_plane[:].bitcast(I32), 0)
+
+        def load_rows(name, rows):
+            raw = sb.tile([P, PACK, rows.shape[1]], F32, name=name)
+            nc.sync.dma_start(out=raw[:], in_=rows.rearrange("(p j) c -> p j c", j=PACK))
+            return raw
+
+        def load_x(z):
+            table = sb.tile([P, T], U32, name="x_table%d" % z, align_bytes=64)
+            nc.sync.dma_start(
+                out=table[:].bitcast(I32),
+                in_=x_words[z].rearrange("p c r -> p (c r)").bitcast(I32),
+            )
+            return table
+
+        w_raw = [None] * 5
+        x_table = [None] * 2
+        w_raw[0] = load_rows("w1_raw0", w1[0:K_PASS, :])
+        nc.sync.dma_start(offsets[:], offs)
+        for q in range(4):
+            nc.sync.dma_start(
+                out=x_plane[32 * q : 32 * q + 8, :].bitcast(I32),
+                in_=x_scales[:, 4 * q : 4 * q + 4, :].bitcast(I32),
+            )
+        x_table[0] = load_x(0)
+        w_raw[1] = load_rows("w2_raw0", w2[0:K_PASS, :])
+        x_table[1] = load_x(1)
+        w_raw[2] = load_rows("w1_raw1", w1[K_PASS:K, :])
+        w_raw[3] = load_rows("w2_raw1", w2[K_PASS:K, :])
+        w_raw[4] = load_rows("w3_raw", w3)
+        e_raw = {}
+        for chunks in E_LOADS:
+            piece = load_rows("e_raw%d" % chunks[0], eT[:, chunks[0] * CHUNK : (chunks[-1] + 1) * CHUNK])
+            for c in chunks:
+                e_raw[c] = piece[:, :, (c - chunks[0]) * CHUNK : (c - chunks[0] + 1) * CHUNK]
+        w4_raw = load_rows("w4_raw", w4)
+
+        def quantize_first_weight(g):
+            grouped = sb.tile([P, PACK, P, PACK], BF16, name="w_grouped%d" % g, align_bytes=64)
+            dst = grouped[:].rearrange("p t m j -> p m j t")
+            src = w_raw[g][:].rearrange("p j (m t) -> p m j t", t=PACK)
+            share = VECTOR_SHARE[g]
+            if share > 0:
+                cast(True, dst[:, 0:share], src[:, 0:share])
+            cast(False, dst[:, share:P], src[:, share:P])
+            return quantize("w%d" % g, grouped[:].rearrange("p t m j -> p (t m j)"), H)
+
+        def quantize_plain(name, raw, on_vector):
+            grouped = sb.tile([P, CHUNK, PACK], BF16, name=name + "_grouped", align_bytes=64)
+            cast(
+                on_vector,
+                grouped[:].rearrange("p (c i) j -> p c j i", i=4),
+                raw.rearrange("p j (c i) -> p c j i", i=4),
+            )
+            return quantize(name, grouped[:].rearrange("p c j -> p (c j)"), CHUNK)
+
+        x_picked_plane = sb.tile([P, S], U8, name="x_picked_plane", align_bytes=64)
+        nc.vector.tensor_copy(x_picked_plane[:], x_plane[:].indirect(offsets[:]))
+
+        def gather_words(z, side):
+            picked = sb.tile([P, V], U32, name="x_picked%d%d" % (z, side), align_bytes=64)
+            nc.vector.tensor_copy(picked[:], x_table[z][:].indirect(offsets[:, side * (V // 16) : (side + 1) * (V // 16)]))
+            return picked
+
+        banks = [ps.tile([P, PACK, CHUNK], F32, name="h_bank%d" % c) for c in range(CHUNKS)]
+
+        def first_layer_pass(c, w, rhs, rhs_scale, first, last):
+            codes, scales = w
+            for t in range(PACK):
+                cols = slice(t * P, (t + 1) * P)
+                nc.tensor.matmul_mx(
+                    out=banks[c][:, t, :],
+                    lhsT=codes[:, cols].bitcast(FP8X4),
+                    lhsT_scale=scales[:, cols],
+                    rhs=rhs.bitcast(FP8X4),
+                    rhs_scale=rhs_scale,
+                    start=(first and t == 0),
+                    stop=(last and t == PACK - 1),
+                )
+
+        for g in range(4):
+            z, side = divmod(g, 2)
+            picked = gather_words(z, side)
+            w = quantize_first_weight(g)
+            for c in range(CHUNKS):
+                first_layer_pass(
+                    c, w, picked[:, c * CHUNK : (c + 1) * CHUNK],
+                    x_picked_plane[4 * z : P, side * V + c * CHUNK : side * V + (c + 1) * CHUNK],
+                    g == 0, False,
+                )
+        w3_q = quantize_first_weight(4)
+
+        for c in range(CHUNKS):
+            e_codes, e_scales = quantize_plain("e%d" % c, e_raw[c], E_CAST_ON_VECTOR[c])
+            first_layer_pass(c, w3_q, e_codes[:], e_scales[:], False, True)
+
+        w4_codes, w4_scales = quantize_plain("w4", w4_raw[:], True)
+
+        h_grouped = []
+        for c in range(CHUNKS):
+            grouped = sb.tile([P, CHUNK, PACK], BF16, name="h_grouped%d" % c, align_bytes=64)
+            src = banks[c][:].rearrange("p t v -> p v t")
+            if RELU_ON_VECTOR[c]:
+                nc.vector.tensor_scalar_max(out=grouped[:], in0=src, scalar1=0.0)
+            else:
+                nc.scalar.activation(out=grouped[:], in_=src, func=ACT.Relu)
+            h_grouped.append(grouped)
+
+        for c in range(CHUNKS):
+            h_codes, h_scales = quantize("h%d" % c, h_grouped[c][:].rearrange("p v t -> p (v t)"), CHUNK)
+            acc = ps.tile([P, CHUNK], F32, name="out_bank%d" % c)
+            nc.tensor.matmul_mx(
+                out=acc[:],
+                lhsT=w4_codes[:].bitcast(FP8X4),
+                lhsT_scale=w4_scales[:],
+                rhs=h_codes[:].bitcast(FP8X4),
+                rhs_scale=h_scales[:],
+                start=True,
+                stop=True,
+            )
+            result = sb.tile([P, CHUNK], F32, name="result%d" % c)
+            cast(OUT_ON_VECTOR[c], result[:], acc[:])
+            nc.sync.dma_start(out=out[:, c * CHUNK : (c + 1) * CHUNK], in_=result[:])

@@ -19,11 +19,12 @@ PACK = 4
 K_PASS = P * PACK
 CHUNK = 128
 CHUNKS = V // CHUNK
-E_LOADS = [[0,1],[2,3]]
-VECTOR_SHARE = [0,0,48,80,88]
-E_CAST_ON_VECTOR = [1,0,1,0]
+E_LOADS = [[0,1,2],[3]]
+VECTOR_SHARE = [0,0,32,64,80]
+E_CAST_ON_VECTOR = [80,80,80,80]
 RELU_ON_VECTOR = [0,0,1,0]
-OUT_ON_VECTOR = [1,1,0,1]
+SECOND_GROUPS = [[0],[1],[2],[3]]
+OUT_ON_VECTOR = [0,0,0,0]
 
 
 def tile_picked_edgeup_relu_p_kernel(tc, x_words, x_scales, eT, w1, w2, w3, w4, offs, out):
@@ -66,7 +67,7 @@ def tile_picked_edgeup_relu_p_kernel(tc, x_words, x_scales, eT, w1, w2, w3, w4, 
         w_raw[0] = load_rows("w1_raw0", w1[0:K_PASS, :])
         nc.sync.dma_start(offsets[:], offs)
         for q in range(4):
-            nc.sync.dma_start(
+            nc.gpsimd.dma_start(
                 out=x_plane[32 * q : 32 * q + 8, :].bitcast(I32),
                 in_=x_scales[:, 4 * q : 4 * q + 4, :].bitcast(I32),
             )
@@ -93,13 +94,14 @@ def tile_picked_edgeup_relu_p_kernel(tc, x_words, x_scales, eT, w1, w2, w3, w4, 
             cast(False, dst[:, share:P], src[:, share:P])
             return quantize("w%d" % g, grouped[:].rearrange("p t m j -> p (t m j)"), H)
 
-        def quantize_plain(name, raw, on_vector):
+        def quantize_plain(name, raw, share):
             grouped = sb.tile([P, CHUNK, PACK], BF16, name=name + "_grouped", align_bytes=64)
-            cast(
-                on_vector,
-                grouped[:].rearrange("p (c i) j -> p c j i", i=4),
-                raw.rearrange("p j (c i) -> p c j i", i=4),
-            )
+            dst = grouped[:].rearrange("p (c i) j -> p c j i", i=4)
+            src = raw.rearrange("p j (c i) -> p c j i", i=4)
+            if share > 0:
+                cast(True, dst[:, 0 : share // 4], src[:, 0 : share // 4])
+            if share < CHUNK:
+                cast(False, dst[:, share // 4 : CHUNK // 4], src[:, share // 4 : CHUNK // 4])
             return quantize(name, grouped[:].rearrange("p c j -> p (c j)"), CHUNK)
 
         x_picked_plane = sb.tile([P, S], U8, name="x_picked_plane", align_bytes=64)
@@ -142,21 +144,25 @@ def tile_picked_edgeup_relu_p_kernel(tc, x_words, x_scales, eT, w1, w2, w3, w4, 
             e_codes, e_scales = quantize_plain("e%d" % c, e_raw[c], E_CAST_ON_VECTOR[c])
             first_layer_pass(c, w3_q, e_codes[:], e_scales[:], False, True)
 
-        w4_codes, w4_scales = quantize_plain("w4", w4_raw[:], True)
+        w4_codes, w4_scales = quantize_plain("w4", w4_raw[:], 128)
 
-        h_grouped = []
-        for c in range(CHUNKS):
-            grouped = sb.tile([P, CHUNK, PACK], BF16, name="h_grouped%d" % c, align_bytes=64)
-            src = banks[c][:].rearrange("p t v -> p v t")
-            if RELU_ON_VECTOR[c]:
-                nc.vector.tensor_scalar_max(out=grouped[:], in0=src, scalar1=0.0)
-            else:
-                nc.scalar.activation(out=grouped[:], in_=src, func=ACT.Relu)
-            h_grouped.append(grouped)
+        h_grouped = {}
+        for group in SECOND_GROUPS:
+            grouped = sb.tile([P, len(group) * CHUNK, PACK], BF16, name="h_grouped%d" % group[0], align_bytes=64)
+            h_grouped[group[0]] = grouped
+            for c in group:
+                dst = grouped[:, (c - group[0]) * CHUNK : (c - group[0] + 1) * CHUNK, :]
+                src = banks[c][:].rearrange("p t v -> p v t")
+                if RELU_ON_VECTOR[c]:
+                    nc.vector.tensor_scalar_max(out=dst, in0=src, scalar1=0.0)
+                else:
+                    nc.scalar.activation(out=dst, in_=src, func=ACT.Relu)
 
-        for c in range(CHUNKS):
-            h_codes, h_scales = quantize("h%d" % c, h_grouped[c][:].rearrange("p v t -> p (v t)"), CHUNK)
-            acc = ps.tile([P, CHUNK], F32, name="out_bank%d" % c)
+        for n, group in enumerate(SECOND_GROUPS):
+            first = group[0]
+            width = len(group) * CHUNK
+            h_codes, h_scales = quantize("h%d" % first, h_grouped[first][:].rearrange("p v t -> p (v t)"), width)
+            acc = ps.tile([P, width], F32, name="out_bank%d" % first)
             nc.tensor.matmul_mx(
                 out=acc[:],
                 lhsT=w4_codes[:].bitcast(FP8X4),
@@ -166,6 +172,6 @@ def tile_picked_edgeup_relu_p_kernel(tc, x_words, x_scales, eT, w1, w2, w3, w4, 
                 start=True,
                 stop=True,
             )
-            result = sb.tile([P, CHUNK], F32, name="result%d" % c)
-            cast(OUT_ON_VECTOR[c], result[:], acc[:])
-            nc.sync.dma_start(out=out[:, c * CHUNK : (c + 1) * CHUNK], in_=result[:])
+            result = sb.tile([P, width], F32, name="result%d" % first)
+            cast(OUT_ON_VECTOR[n], result[:], acc[:])
+            nc.sync.dma_start(out=out[:, first * CHUNK : first * CHUNK + width], in_=result[:])

@@ -20,7 +20,7 @@ K_PASS = P * PACK
 CHUNK = 128
 CHUNKS = V // CHUNK
 E_LOADS = [[0,1,2],[3]]
-VECTOR_SHARE = [0,0,32,64,80]
+VECTOR_SHARE = [0,48,48,48,80]
 E_CAST_ON_VECTOR = [80,80,80,80]
 RELU_ON_VECTOR = [0,0,1,0]
 SECOND_GROUPS = [[0],[1],[2],[3]]
@@ -64,16 +64,21 @@ def tile_picked_edgeup_relu_p_kernel(tc, x_words, x_scales, eT, w1, w2, w3, w4, 
 
         w_raw = [None] * 5
         x_table = [None] * 2
-        w_raw[0] = load_rows("w1_raw0", w1[0:K_PASS, :])
-        nc.sync.dma_start(offsets[:], offs)
-        for q in range(4):
-            nc.gpsimd.dma_start(
-                out=x_plane[32 * q : 32 * q + 8, :].bitcast(I32),
-                in_=x_scales[:, 4 * q : 4 * q + 4, :].bitcast(I32),
-            )
+        def load_scale_rows(rows):
+            for r in rows:
+                for z in range(2):
+                    nc.sync.dma_start(
+                        out=x_plane[4 * z + r : P : 32, :].bitcast(I32),
+                        in_=x_scales[z, r:16:4, :].bitcast(I32),
+                    )
+
         x_table[0] = load_x(0)
-        w_raw[1] = load_rows("w2_raw0", w2[0:K_PASS, :])
+        nc.sync.dma_start(offsets[:], offs)
+        load_scale_rows((0, 1))
         x_table[1] = load_x(1)
+        w_raw[0] = load_rows("w1_raw0", w1[0:K_PASS, :])
+        load_scale_rows((2, 3))
+        w_raw[1] = load_rows("w2_raw0", w2[0:K_PASS, :])
         w_raw[2] = load_rows("w1_raw1", w1[K_PASS:K, :])
         w_raw[3] = load_rows("w2_raw1", w2[K_PASS:K, :])
         w_raw[4] = load_rows("w3_raw", w3)
@@ -104,13 +109,15 @@ def tile_picked_edgeup_relu_p_kernel(tc, x_words, x_scales, eT, w1, w2, w3, w4, 
                 cast(False, dst[:, share // 4 : CHUNK // 4], src[:, share // 4 : CHUNK // 4])
             return quantize(name, grouped[:].rearrange("p c j -> p (c j)"), CHUNK)
 
-        x_picked_plane = sb.tile([P, S], U8, name="x_picked_plane", align_bytes=64)
-        nc.vector.tensor_copy(x_picked_plane[:], x_plane[:].indirect(offsets[:]))
 
         def gather_words(z, side):
             picked = sb.tile([P, V], U32, name="x_picked%d%d" % (z, side), align_bytes=64)
             nc.vector.tensor_copy(picked[:], x_table[z][:].indirect(offsets[:, side * (V // 16) : (side + 1) * (V // 16)]))
             return picked
+
+        x_picked = [gather_words(z, side) for z in range(2) for side in range(2)]
+        x_picked_plane = sb.tile([P, S], U8, name="x_picked_plane", align_bytes=64)
+        nc.vector.tensor_copy(x_picked_plane[:], x_plane[:].indirect(offsets[:]))
 
         banks = [ps.tile([P, PACK, CHUNK], F32, name="h_bank%d" % c) for c in range(CHUNKS)]
 
@@ -130,7 +137,7 @@ def tile_picked_edgeup_relu_p_kernel(tc, x_words, x_scales, eT, w1, w2, w3, w4, 
 
         for g in range(4):
             z, side = divmod(g, 2)
-            picked = gather_words(z, side)
+            picked = x_picked[g]
             w = quantize_first_weight(g)
             for c in range(CHUNKS):
                 first_layer_pass(

@@ -19,11 +19,12 @@ PACK = 4
 K_PASS = P * PACK
 CHUNK = 128
 CHUNKS = V // CHUNK
-E_LOADS = [[0,1,2],[3]]
-VECTOR_SHARE = [0,48,48,48,80]
-E_CAST_ON_VECTOR = [80,80,80,80]
+E_LOADS = [[0],[1,2],[3]]
+W_SHARE = [0,48,48,48,80]
+E_SHARE = [0,128,0,0]
+W4_SHARE = 128
 RELU_ON_VECTOR = [0,0,1,0]
-SECOND_GROUPS = [[0],[1],[2],[3]]
+HELD = 2
 OUT_ON_VECTOR = [0,0,0,0]
 
 
@@ -39,20 +40,28 @@ def tile_picked_edgeup_relu_p_kernel(tc, x_words, x_scales, eT, w1, w2, w3, w4, 
             else:
                 nc.scalar.activation(out=dst, in_=src, func=ACT.Copy)
 
-        def quantize(name, grouped, width):
+        def shared_cast(dst, src, share, whole):
+            if share > 0:
+                cast(True, dst[:, 0:share], src[:, 0:share])
+            if share < whole:
+                cast(False, dst[:, share:whole], src[:, share:whole])
+
+        def quantize(name, grouped, width, scales=None):
             codes = sb.tile([P, width], U32, name=name + "_codes", align_bytes=64)
-            scales = sb.tile([P, width], U8, name=name + "_scales", align_bytes=64)
-            nc.vector.quantize_mx(out=codes[:].bitcast(FP8X4), scales=scales[:], in_=grouped)
-            return codes, scales
+            if scales is None:
+                scales = sb.tile([P, width], U8, name=name + "_scales", align_bytes=64)[:]
+            nc.vector.quantize_mx(out=codes[:].bitcast(FP8X4), scales=scales, in_=grouped)
+            return codes[:], scales
 
         offsets = sb.tile([P, S // 16], U16, name="offsets")
         x_plane = sb.tile([P, T], U8, name="x_plane", align_bytes=64)
         nc.gpsimd.memset(x_plane[:].bitcast(I32), 0)
 
         def load_rows(name, rows):
-            raw = sb.tile([P, PACK, rows.shape[1]], F32, name=name)
-            nc.sync.dma_start(out=raw[:], in_=rows.rearrange("(p j) c -> p j c", j=PACK))
-            return raw
+            passes = rows.shape[0] // K_PASS
+            raw = sb.tile([P, passes, PACK, rows.shape[1]], F32, name=name)
+            nc.sync.dma_start(out=raw[:], in_=rows.rearrange("(z p j) c -> p z j c", j=PACK, p=P))
+            return [raw[:, z] for z in range(passes)]
 
         def load_x(z):
             table = sb.tile([P, T], U32, name="x_table%d" % z, align_bytes=64)
@@ -62,8 +71,6 @@ def tile_picked_edgeup_relu_p_kernel(tc, x_words, x_scales, eT, w1, w2, w3, w4, 
             )
             return table
 
-        w_raw = [None] * 5
-        x_table = [None] * 2
         def load_scale_rows(rows):
             for r in rows:
                 for z in range(2):
@@ -72,113 +79,123 @@ def tile_picked_edgeup_relu_p_kernel(tc, x_words, x_scales, eT, w1, w2, w3, w4, 
                         in_=x_scales[z, r:16:4, :].bitcast(I32),
                     )
 
-        x_table[0] = load_x(0)
+        x_table = [load_x(0)]
         nc.sync.dma_start(offsets[:], offs)
         load_scale_rows((0, 1))
-        x_table[1] = load_x(1)
-        w_raw[0] = load_rows("w1_raw0", w1[0:K_PASS, :])
+        x_table.append(load_x(1))
+        (w1a,) = load_rows("w1a", w1[0:K_PASS, :])
         load_scale_rows((2, 3))
-        w_raw[1] = load_rows("w2_raw0", w2[0:K_PASS, :])
-        w_raw[2] = load_rows("w1_raw1", w1[K_PASS:K, :])
-        w_raw[3] = load_rows("w2_raw1", w2[K_PASS:K, :])
-        w_raw[4] = load_rows("w3_raw", w3)
+        (w2a,) = load_rows("w2a", w2[0:K_PASS, :])
+        (w1b,) = load_rows("w1b", w1[K_PASS:K, :])
+        (w2b,) = load_rows("w2b", w2[K_PASS:K, :])
+        node_passes = [(w1a, 0, 0), (w2a, 0, 1), (w1b, 1, 0), (w2b, 1, 1)]
+        (w3_raw,) = load_rows("w3_raw", w3)
         e_raw = {}
         for chunks in E_LOADS:
-            piece = load_rows("e_raw%d" % chunks[0], eT[:, chunks[0] * CHUNK : (chunks[-1] + 1) * CHUNK])
+            (piece,) = load_rows("e_raw%d" % chunks[0], eT[:, chunks[0] * CHUNK : (chunks[-1] + 1) * CHUNK])
             for c in chunks:
                 e_raw[c] = piece[:, :, (c - chunks[0]) * CHUNK : (c - chunks[0] + 1) * CHUNK]
-        w4_raw = load_rows("w4_raw", w4)
+        (w4_raw,) = load_rows("w4_raw", w4)
 
-        def quantize_first_weight(g):
+        def round_first_weight(g, raw):
             grouped = sb.tile([P, PACK, P, PACK], BF16, name="w_grouped%d" % g, align_bytes=64)
             dst = grouped[:].rearrange("p t m j -> p m j t")
-            src = w_raw[g][:].rearrange("p j (m t) -> p m j t", t=PACK)
-            share = VECTOR_SHARE[g]
-            if share > 0:
-                cast(True, dst[:, 0:share], src[:, 0:share])
-            cast(False, dst[:, share:P], src[:, share:P])
-            return quantize("w%d" % g, grouped[:].rearrange("p t m j -> p (t m j)"), H)
+            src = raw.rearrange("p j (m t) -> p m j t", t=PACK)
+            shared_cast(dst, src, W_SHARE[g], P)
+            return grouped[:].rearrange("p t m j -> p (t m j)")
 
-        def quantize_plain(name, raw, share):
+        def round_plain(name, raw, share):
             grouped = sb.tile([P, CHUNK, PACK], BF16, name=name + "_grouped", align_bytes=64)
             dst = grouped[:].rearrange("p (c i) j -> p c j i", i=4)
             src = raw.rearrange("p j (c i) -> p c j i", i=4)
-            if share > 0:
-                cast(True, dst[:, 0 : share // 4], src[:, 0 : share // 4])
-            if share < CHUNK:
-                cast(False, dst[:, share // 4 : CHUNK // 4], src[:, share // 4 : CHUNK // 4])
-            return quantize(name, grouped[:].rearrange("p c j -> p (c j)"), CHUNK)
-
+            shared_cast(dst, src, share // 4, CHUNK // 4)
+            return grouped[:].rearrange("p c j -> p (c j)")
 
         def gather_words(z, side):
             picked = sb.tile([P, V], U32, name="x_picked%d%d" % (z, side), align_bytes=64)
             nc.vector.tensor_copy(picked[:], x_table[z][:].indirect(offsets[:, side * (V // 16) : (side + 1) * (V // 16)]))
             return picked
 
-        x_picked = [gather_words(z, side) for z in range(2) for side in range(2)]
+        x_picked = [[gather_words(z, side) for side in range(2)] for z in range(2)]
         x_picked_plane = sb.tile([P, S], U8, name="x_picked_plane", align_bytes=64)
         nc.vector.tensor_copy(x_picked_plane[:], x_plane[:].indirect(offsets[:]))
 
         banks = [ps.tile([P, PACK, CHUNK], F32, name="h_bank%d" % c) for c in range(CHUNKS)]
 
-        def first_layer_pass(c, w, rhs, rhs_scale, first, last):
+        def column_tiles(w):
             codes, scales = w
-            for t in range(PACK):
-                cols = slice(t * P, (t + 1) * P)
+            return [(codes[:, first : first + P], scales[:, first : first + P]) for first in range(0, codes.shape[1], P)]
+
+        def first_layer_pass(c, tiles, rhs, rhs_scale, first, last):
+            for t, (codes, scales) in enumerate(tiles):
                 nc.tensor.matmul_mx(
                     out=banks[c][:, t, :],
-                    lhsT=codes[:, cols].bitcast(FP8X4),
-                    lhsT_scale=scales[:, cols],
+                    lhsT=codes.bitcast(FP8X4),
+                    lhsT_scale=scales,
                     rhs=rhs.bitcast(FP8X4),
                     rhs_scale=rhs_scale,
                     start=(first and t == 0),
                     stop=(last and t == PACK - 1),
                 )
 
-        for g in range(4):
-            z, side = divmod(g, 2)
-            picked = x_picked[g]
-            w = quantize_first_weight(g)
+        def node_pass(g, tiles, c):
+            z, side = node_passes[g][1:]
+            first_layer_pass(
+                c, tiles, x_picked[z][side][:, c * CHUNK : (c + 1) * CHUNK],
+                x_picked_plane[4 * z : P, side * V + c * CHUNK : side * V + (c + 1) * CHUNK],
+                g == 0, False,
+            )
+
+        for g in range(3):
+            tiles = column_tiles(quantize("w%d" % g, round_first_weight(g, node_passes[g][0]), H))
             for c in range(CHUNKS):
-                first_layer_pass(
-                    c, w, picked[:, c * CHUNK : (c + 1) * CHUNK],
-                    x_picked_plane[4 * z : P, side * V + c * CHUNK : side * V + (c + 1) * CHUNK],
-                    g == 0, False,
-                )
-        w3_q = quantize_first_weight(4)
-
-        for c in range(CHUNKS):
-            e_codes, e_scales = quantize_plain("e%d" % c, e_raw[c], E_CAST_ON_VECTOR[c])
-            first_layer_pass(c, w3_q, e_codes[:], e_scales[:], False, True)
-
-        w4_codes, w4_scales = quantize_plain("w4", w4_raw[:], 128)
+                node_pass(g, tiles, c)
+        shared_scales = sb.tile([P, H], U8, name="shared_scales", align_bytes=64)
+        last_tiles = column_tiles(quantize("w3", round_first_weight(3, node_passes[3][0]), H, shared_scales[:]))
+        for c in range(CHUNKS - HELD):
+            node_pass(3, last_tiles, c)
+        w3_grouped = round_first_weight(4, w3_raw)
+        half = H // 2
+        w3_q = column_tiles(quantize("w4a", w3_grouped[:, 0 : PACK * half], half, shared_scales[4:P, 0:half]))
+        for c in range(CHUNKS - HELD, CHUNKS):
+            node_pass(3, last_tiles, c)
+        w3_q = w3_q + column_tiles(quantize("w4b", w3_grouped[:, PACK * half : PACK * H], half))
 
         h_grouped = {}
-        for group in SECOND_GROUPS:
-            grouped = sb.tile([P, len(group) * CHUNK, PACK], BF16, name="h_grouped%d" % group[0], align_bytes=64)
-            h_grouped[group[0]] = grouped
-            for c in group:
-                dst = grouped[:, (c - group[0]) * CHUNK : (c - group[0] + 1) * CHUNK, :]
-                src = banks[c][:].rearrange("p t v -> p v t")
-                if RELU_ON_VECTOR[c]:
-                    nc.vector.tensor_scalar_max(out=dst, in0=src, scalar1=0.0)
-                else:
-                    nc.scalar.activation(out=dst, in_=src, func=ACT.Relu)
 
-        for n, group in enumerate(SECOND_GROUPS):
-            first = group[0]
-            width = len(group) * CHUNK
-            h_codes, h_scales = quantize("h%d" % first, h_grouped[first][:].rearrange("p v t -> p (v t)"), width)
-            acc = ps.tile([P, width], F32, name="out_bank%d" % first)
+        def edge_pass(c):
+            e_codes, e_scales = quantize("e%d" % c, round_plain("e%d" % c, e_raw[c], E_SHARE[c]), CHUNK)
+            first_layer_pass(c, w3_q, e_codes, e_scales, False, True)
+
+        def relu(c):
+            grouped = sb.tile([P, CHUNK, PACK], BF16, name="h_grouped%d" % c, align_bytes=64)
+            h_grouped[c] = grouped
+            src = banks[c][:].rearrange("p t v -> p v t")
+            if RELU_ON_VECTOR[c]:
+                nc.vector.tensor_scalar_max(out=grouped[:], in0=src, scalar1=0.0)
+            else:
+                nc.scalar.activation(out=grouped[:], in_=src, func=ACT.Relu)
+
+        def second_layer(c, w4_q):
+            h_codes, h_scales = quantize("h%d" % c, h_grouped[c][:].rearrange("p v t -> p (v t)"), CHUNK)
+            acc = ps.tile([P, CHUNK], F32, name="out_bank%d" % c)
             nc.tensor.matmul_mx(
                 out=acc[:],
-                lhsT=w4_codes[:].bitcast(FP8X4),
-                lhsT_scale=w4_scales[:],
-                rhs=h_codes[:].bitcast(FP8X4),
-                rhs_scale=h_scales[:],
+                lhsT=w4_q[0].bitcast(FP8X4),
+                lhsT_scale=w4_q[1],
+                rhs=h_codes.bitcast(FP8X4),
+                rhs_scale=h_scales,
                 start=True,
                 stop=True,
             )
-            result = sb.tile([P, width], F32, name="result%d" % first)
-            cast(OUT_ON_VECTOR[n], result[:], acc[:])
-            nc.sync.dma_start(out=out[:, first * CHUNK : first * CHUNK + width], in_=result[:])
+            result = sb.tile([P, CHUNK], F32, name="result%d" % c)
+            cast(OUT_ON_VECTOR[c], result[:], acc[:])
+            nc.sync.dma_start(out=out[:, c * CHUNK : (c + 1) * CHUNK], in_=result[:])
+
+        for c in range(CHUNKS):
+            edge_pass(c)
+        w4_q = quantize("w4", round_plain("w4", w4_raw, W4_SHARE), CHUNK)
+        for c in range(CHUNKS):
+            relu(c)
+        for c in range(CHUNKS):
+            second_layer(c, w4_q)

@@ -20,7 +20,7 @@ K_PASS = P * PACK
 CHUNK = 128
 CHUNKS = V // CHUNK
 E_LOADS = [[0],[1,2],[3]]
-W_SHARE = [0,48,48,48,80]
+W_SHARE = [0,48,48,64,80]
 E_SHARE = [0,128,0,0]
 W4_SHARE = 128
 RELU_ON_VECTOR = [0,0,1,0]

@@ -19,11 +19,12 @@ PACK = 4
 K_PASS = P * PACK
 CHUNK = 128
 CHUNKS = V // CHUNK
-E_LOADS = [[0],[1,2],[3]]
+E_LOADS = [[0],[1],[2],[3]]
 W_SHARE = [0,48,48,64,80]
-E_SHARE = [0,128,0,0]
+E_SHARE = [0,128,0,128]
 W4_SHARE = 128
 RELU_ON_VECTOR = [0,0,1,0]
+STORES = [[0],[1],[2,3]]
 HELD = 2
 OUT_ON_VECTOR = [0,0,0,0]
 
@@ -90,11 +91,14 @@ def tile_picked_edgeup_relu_p_kernel(tc, x_words, x_scales, eT, w1, w2, w3, w4, 
         (w2b,) = load_rows("w2b", w2[K_PASS:K, :])
         node_passes = [(w1a, 0, 0), (w2a, 0, 1), (w1b, 1, 0), (w2b, 1, 1)]
         (w3_raw,) = load_rows("w3_raw", w3)
-        e_raw = {}
+        e_pairs = sb.tile([P, 2, 2 * V], F32, name="e_pairs")
+        e_rows = eT.rearrange("(p u j) c -> p u (j c)", u=2, j=2)
         for chunks in E_LOADS:
-            (piece,) = load_rows("e_raw%d" % chunks[0], eT[:, chunks[0] * CHUNK : (chunks[-1] + 1) * CHUNK])
-            for c in chunks:
-                e_raw[c] = piece[:, :, (c - chunks[0]) * CHUNK : (c - chunks[0] + 1) * CHUNK]
+            first = V + chunks[0] * CHUNK if chunks[0] > 0 else 0
+            last = V + (chunks[-1] + 1) * CHUNK
+            nc.sync.dma_start(out=e_pairs[:, :, first:last], in_=e_rows[:, :, first:last])
+        e_all = e_pairs[:].rearrange("p u (j c) -> p (u j) c", j=2)
+        e_raw = [e_all[:, :, c * CHUNK : (c + 1) * CHUNK] for c in range(CHUNKS)]
         (w4_raw,) = load_rows("w4_raw", w4)
 
         def round_first_weight(g, raw):
@@ -162,6 +166,7 @@ def tile_picked_edgeup_relu_p_kernel(tc, x_words, x_scales, eT, w1, w2, w3, w4, 
         w3_q = w3_q + column_tiles(quantize("w4b", w3_grouped[:, PACK * half : PACK * H], half))
 
         h_grouped = {}
+        results = {}
 
         def edge_pass(c):
             e_codes, e_scales = quantize("e%d" % c, round_plain("e%d" % c, e_raw[c], E_SHARE[c]), CHUNK)
@@ -188,9 +193,13 @@ def tile_picked_edgeup_relu_p_kernel(tc, x_words, x_scales, eT, w1, w2, w3, w4, 
                 start=True,
                 stop=True,
             )
-            result = sb.tile([P, CHUNK], F32, name="result%d" % c)
-            cast(OUT_ON_VECTOR[c], result[:], acc[:])
-            nc.sync.dma_start(out=out[:, c * CHUNK : (c + 1) * CHUNK], in_=result[:])
+            (group,) = [chunks for chunks in STORES if c in chunks]
+            if c == group[0]:
+                results[c] = sb.tile([P, len(group) * CHUNK], F32, name="result%d" % c)
+            result = results[group[0]]
+            cast(OUT_ON_VECTOR[c], result[:, (c - group[0]) * CHUNK : (c - group[0] + 1) * CHUNK], acc[:])
+            if c == group[-1]:
+                nc.sync.dma_start(out=out[:, group[0] * CHUNK : (c + 1) * CHUNK], in_=result[:])
 
         for c in range(CHUNKS):
             edge_pass(c)

@@ -23,8 +23,8 @@ E_LOADS = [[0],[1],[2],[3]]
 W_SHARE = [0,48,48,64,80]
 E_SHARE = [0,128,0,128]
 W4_SHARE = 128
-RELU_ON_VECTOR = [0,0,1,0]
-STORES = [[0],[1],[2,3]]
+RELU_ON_VECTOR = [0,1,0,0]
+STORES = [[0,1],[2],[3]]
 HELD = 2
 OUT_ON_VECTOR = [0,0,0,0]
 
@@ -109,7 +109,7 @@ def tile_picked_edgeup_relu_p_kernel(tc, x_words, x_scales, eT, w1, w2, w3, w4, 
             return grouped[:].rearrange("p t m j -> p (t m j)")
 
         def round_plain(name, raw, share):
-            grouped = sb.tile([P, CHUNK, PACK], BF16, name=name + "_grouped", align_bytes=64)
+            grouped = sb.tile([P, CHUNK, PACK], BF16, name=name + "_grouped", tag=name + "_grouped", align_bytes=64)
             dst = grouped[:].rearrange("p (c i) j -> p c j i", i=4)
             src = raw.rearrange("p j (c i) -> p c j i", i=4)
             shared_cast(dst, src, share // 4, CHUNK // 4)
@@ -173,7 +173,7 @@ def tile_picked_edgeup_relu_p_kernel(tc, x_words, x_scales, eT, w1, w2, w3, w4, 
             first_layer_pass(c, w3_q, e_codes, e_scales, False, True)
 
         def relu(c):
-            grouped = sb.tile([P, CHUNK, PACK], BF16, name="h_grouped%d" % c, align_bytes=64)
+            grouped = sb.tile([P, CHUNK, PACK], BF16, name="h_grouped%d" % c, tag="e3_grouped" if c == 1 else "h_grouped%d" % c, align_bytes=64)
             h_grouped[c] = grouped
             src = banks[c][:].rearrange("p t v -> p v t")
             if RELU_ON_VECTOR[c]:

@@ -20,7 +20,7 @@ K_PASS = P * PACK
 CHUNK = 128
 CHUNKS = V // CHUNK
 E_LOADS = [[0],[1],[2],[3]]
-W_SHARE = [0,48,48,64,80]
+W_SHARE = [0,48,64,64,80]
 E_SHARE = [0,128,0,128]
 W4_SHARE = 128
 RELU_ON_VECTOR = [0,1,0,0]
@@ -55,8 +55,11 @@ def tile_picked_edgeup_relu_p_kernel(tc, x_words, x_scales, eT, w1, w2, w3, w4, 
             return codes[:], scales
 
         offsets = sb.tile([P, S // 16], U16, name="offsets")
-        x_plane = sb.tile([P, T], U8, name="x_plane", align_bytes=64)
-        nc.gpsimd.memset(x_plane[:].bitcast(I32), 0)
+        scale_rows = sb.tile([P, T], U8, name="scale_rows", align_bytes=64)
+        x_picked_plane = sb.tile([P, S], U8, name="x_picked_plane", align_bytes=64)
+        nc.gpsimd.memset(scale_rows[32:64, :].bitcast(I32), 0)
+        nc.gpsimd.memset(scale_rows[64:P, :].bitcast(I32), 0)
+        nc.gpsimd.memset(x_picked_plane[:].bitcast(I32), 0)
 
         def load_rows(name, rows):
             passes = rows.shape[0] // K_PASS
@@ -64,29 +67,30 @@ def tile_picked_edgeup_relu_p_kernel(tc, x_words, x_scales, eT, w1, w2, w3, w4, 
             nc.sync.dma_start(out=raw[:], in_=rows.rearrange("(z p j) c -> p z j c", j=PACK, p=P))
             return [raw[:, z] for z in range(passes)]
 
-        def load_x(z):
-            table = sb.tile([P, T], U32, name="x_table%d" % z, align_bytes=64)
+        def load_x():
+            table = sb.tile([P, 2, T], U32, name="x_table", align_bytes=64)
             nc.sync.dma_start(
                 out=table[:].bitcast(I32),
-                in_=x_words[z].rearrange("p c r -> p (c r)").bitcast(I32),
+                in_=x_words.rearrange("z p c r -> p z (c r)").bitcast(I32),
             )
-            return table
+            return [table[:, z, :] for z in range(2)]
 
-        def load_scale_rows(rows):
-            for r in rows:
-                for z in range(2):
-                    nc.sync.dma_start(
-                        out=x_plane[4 * z + r : P : 32, :].bitcast(I32),
-                        in_=x_scales[z, r:16:4, :].bitcast(I32),
-                    )
+        def place_scale_rows(z):
+            for r in range(4):
+                nc.sync.dma_start(
+                    out=x_picked_plane[4 * z + r : P : 32, :].bitcast(I32),
+                    in_=picked_rows[16 * z + r : 16 * (z + 1) : 4, :].bitcast(I32),
+                )
 
-        x_table = [load_x(0)]
+        nc.sync.dma_start(out=scale_rows[0:32, :].bitcast(I32), in_=x_scales.rearrange("z q c -> (z q) c").bitcast(I32))
         nc.sync.dma_start(offsets[:], offs)
-        load_scale_rows((0, 1))
-        x_table.append(load_x(1))
+        picked_rows = sb.tile([P, S], U8, name="picked_rows", align_bytes=64)
+        nc.vector.tensor_copy(picked_rows[:], scale_rows[:].indirect(offsets[:]))
+        x_table = load_x()
         (w1a,) = load_rows("w1a", w1[0:K_PASS, :])
-        load_scale_rows((2, 3))
+        place_scale_rows(0)
         (w2a,) = load_rows("w2a", w2[0:K_PASS, :])
+        place_scale_rows(1)
         (w1b,) = load_rows("w1b", w1[K_PASS:K, :])
         (w2b,) = load_rows("w2b", w2[K_PASS:K, :])
         node_passes = [(w1a, 0, 0), (w2a, 0, 1), (w1b, 1, 0), (w2b, 1, 1)]
@@ -117,12 +121,10 @@ def tile_picked_edgeup_relu_p_kernel(tc, x_words, x_scales, eT, w1, w2, w3, w4, 
 
         def gather_words(z, side):
             picked = sb.tile([P, V], U32, name="x_picked%d%d" % (z, side), align_bytes=64)
-            nc.vector.tensor_copy(picked[:], x_table[z][:].indirect(offsets[:, side * (V // 16) : (side + 1) * (V // 16)]))
+            nc.vector.tensor_copy(picked[:], x_table[z].indirect(offsets[:, side * (V // 16) : (side + 1) * (V // 16)]))
             return picked
 
         x_picked = [[gather_words(z, side) for side in range(2)] for z in range(2)]
-        x_picked_plane = sb.tile([P, S], U8, name="x_picked_plane", align_bytes=64)
-        nc.vector.tensor_copy(x_picked_plane[:], x_plane[:].indirect(offsets[:]))
 
         banks = [ps.tile([P, PACK, CHUNK], F32, name="h_bank%d" % c) for c in range(CHUNKS)]
 

@@ -75,12 +75,13 @@ def tile_picked_edgeup_relu_p_kernel(tc, x_words, x_scales, eT, w1, w2, w3, w4, 
             )
             return [table[:, z, :] for z in range(2)]
 
-        def place_scale_rows(z):
-            for r in range(4):
-                nc.sync.dma_start(
-                    out=x_picked_plane[4 * z + r : P : 32, :].bitcast(I32),
-                    in_=picked_rows[16 * z + r : 16 * (z + 1) : 4, :].bitcast(I32),
-                )
+        def place_scale_rows(rows):
+            for r in rows:
+                for z in range(2):
+                    nc.sync.dma_start(
+                        out=x_picked_plane[4 * z + r : P : 32, :].bitcast(I32),
+                        in_=picked_rows[16 * z + r : 16 * (z + 1) : 4, :].bitcast(I32),
+                    )
 
         nc.sync.dma_start(out=scale_rows[0:32, :].bitcast(I32), in_=x_scales.rearrange("z q c -> (z q) c").bitcast(I32))
         nc.sync.dma_start(offsets[:], offs)
@@ -88,9 +89,9 @@ def tile_picked_edgeup_relu_p_kernel(tc, x_words, x_scales, eT, w1, w2, w3, w4, 
         nc.vector.tensor_copy(picked_rows[:], scale_rows[:].indirect(offsets[:]))
         x_table = load_x()
         (w1a,) = load_rows("w1a", w1[0:K_PASS, :])
-        place_scale_rows(0)
+        place_scale_rows((0, 1))
         (w2a,) = load_rows("w2a", w2[0:K_PASS, :])
-        place_scale_rows(1)
+        place_scale_rows((2, 3))
         (w1b,) = load_rows("w1b", w1[K_PASS:K, :])
         (w2b,) = load_rows("w2b", w2[K_PASS:K, :])
         node_passes = [(w1a, 0, 0), (w2a, 0, 1), (w1b, 1, 0), (w2b, 1, 1)]

@@ -26,6 +26,7 @@ W4_SHARE = 128
 RELU_ON_VECTOR = [0,1,0,0]
 STORES = [[0,1],[2],[3]]
 HELD = 2
+DMA_ALIGN = 256
 OUT_ON_VECTOR = [0,0,0,0]
 
 
@@ -35,17 +36,19 @@ def tile_picked_edgeup_relu_p_kernel(tc, x_words, x_scales, eT, w1, w2, w3, w4, 
         sb = ctx.enter_context(tc.tile_pool(name="sb", bufs=1))
         ps = ctx.enter_context(tc.psum_pool(name="ps", bufs=1))
 
-        def cast(on_vector, dst, src):
+        def cast(on_vector, dst, src, as_activation=False):
             if on_vector:
                 nc.vector.tensor_copy(out=dst, in_=src)
-            else:
+            elif as_activation:
                 nc.scalar.activation(out=dst, in_=src, func=ACT.Copy)
+            else:
+                nc.scalar.copy(out=dst, in_=src)
 
-        def shared_cast(dst, src, share, whole):
+        def shared_cast(dst, src, share, whole, as_activation=False):
             if share > 0:
                 cast(True, dst[:, 0:share], src[:, 0:share])
             if share < whole:
-                cast(False, dst[:, share:whole], src[:, share:whole])
+                cast(False, dst[:, share:whole], src[:, share:whole], as_activation)
 
         def quantize(name, grouped, width, scales=None):
             codes = sb.tile([P, width], U32, name=name + "_codes", align_bytes=64)
@@ -54,21 +57,21 @@ def tile_picked_edgeup_relu_p_kernel(tc, x_words, x_scales, eT, w1, w2, w3, w4, 
             nc.vector.quantize_mx(out=codes[:].bitcast(FP8X4), scales=scales, in_=grouped)
             return codes[:], scales
 
-        offsets = sb.tile([P, S // 16], U16, name="offsets")
-        scale_rows = sb.tile([P, T], U8, name="scale_rows", align_bytes=64)
-        x_picked_plane = sb.tile([P, S], U8, name="x_picked_plane", align_bytes=64)
+        offsets = sb.tile([P, S // 16], U16, name="offsets", align_bytes=DMA_ALIGN)
+        scale_rows = sb.tile([P, T], U8, name="scale_rows", align_bytes=DMA_ALIGN)
+        x_picked_plane = sb.tile([P, S], U8, name="x_picked_plane", align_bytes=DMA_ALIGN)
         nc.gpsimd.memset(scale_rows[32:64, :].bitcast(I32), 0)
         nc.gpsimd.memset(scale_rows[64:P, :].bitcast(I32), 0)
         nc.gpsimd.memset(x_picked_plane[:].bitcast(I32), 0)
 
         def load_rows(name, rows):
             passes = rows.shape[0] // K_PASS
-            raw = sb.tile([P, passes, PACK, rows.shape[1]], F32, name=name)
+            raw = sb.tile([P, passes, PACK, rows.shape[1]], F32, name=name, align_bytes=DMA_ALIGN)
             nc.sync.dma_start(out=raw[:], in_=rows.rearrange("(z p j) c -> p z j c", j=PACK, p=P))
             return [raw[:, z] for z in range(passes)]
 
         def load_x():
-            table = sb.tile([P, 2, T], U32, name="x_table", align_bytes=64)
+            table = sb.tile([P, 2, T], U32, name="x_table", align_bytes=DMA_ALIGN)
             nc.sync.dma_start(
                 out=table[:].bitcast(I32),
                 in_=x_words.rearrange("z p c r -> p z (c r)").bitcast(I32),
@@ -85,7 +88,7 @@ def tile_picked_edgeup_relu_p_kernel(tc, x_words, x_scales, eT, w1, w2, w3, w4, 
 
         nc.sync.dma_start(out=scale_rows[0:32, :].bitcast(I32), in_=x_scales.rearrange("z q c -> (z q) c").bitcast(I32))
         nc.sync.dma_start(offsets[:], offs)
-        picked_rows = sb.tile([P, S], U8, name="picked_rows", align_bytes=64)
+        picked_rows = sb.tile([P, S], U8, name="picked_rows", align_bytes=DMA_ALIGN)
         nc.vector.tensor_copy(picked_rows[:], scale_rows[:].indirect(offsets[:]))
         x_table = load_x()
         (w1a,) = load_rows("w1a", w1[0:K_PASS, :])
@@ -96,7 +99,7 @@ def tile_picked_edgeup_relu_p_kernel(tc, x_words, x_scales, eT, w1, w2, w3, w4, 
         (w2b,) = load_rows("w2b", w2[K_PASS:K, :])
         node_passes = [(w1a, 0, 0), (w2a, 0, 1), (w1b, 1, 0), (w2b, 1, 1)]
         (w3_raw,) = load_rows("w3_raw", w3)
-        e_pairs = sb.tile([P, 2, 2 * V], F32, name="e_pairs")
+        e_pairs = sb.tile([P, 2, 2 * V], F32, name="e_pairs", align_bytes=DMA_ALIGN)
         e_rows = eT.rearrange("(p u j) c -> p u (j c)", u=2, j=2)
         for chunks in E_LOADS:
             first = V + chunks[0] * CHUNK if chunks[0] > 0 else 0
@@ -110,7 +113,7 @@ def tile_picked_edgeup_relu_p_kernel(tc, x_words, x_scales, eT, w1, w2, w3, w4, 
             grouped = sb.tile([P, PACK, P, PACK], BF16, name="w_grouped%d" % g, align_bytes=64)
             dst = grouped[:].rearrange("p t m j -> p m j t")
             src = raw.rearrange("p j (m t) -> p m j t", t=PACK)
-            shared_cast(dst, src, W_SHARE[g], P)
+            shared_cast(dst, src, W_SHARE[g], P, g == 0)
             return grouped[:].rearrange("p t m j -> p (t m j)")
 
         def round_plain(name, raw, share):
@@ -198,7 +201,7 @@ def tile_picked_edgeup_relu_p_kernel(tc, x_words, x_scales, eT, w1, w2, w3, w4, 
             )
             (group,) = [chunks for chunks in STORES if c in chunks]
             if c == group[0]:
-                results[c] = sb.tile([P, len(group) * CHUNK], F32, name="result%d" % c)
+                results[c] = sb.tile([P, len(group) * CHUNK], F32, name="result%d" % c, align_bytes=DMA_ALIGN)
             result = results[group[0]]
             cast(OUT_ON_VECTOR[c], result[:, (c - group[0]) * CHUNK : (c - group[0] + 1) * CHUNK], acc[:])
             if c == group[-1]:

@@ -23,7 +23,7 @@ E_LOADS = [[0],[1],[2],[3]]
 W_SHARE = [0,48,64,64,80]
 E_SHARE = [0,128,0,128]
 W4_SHARE = 128
-RELU_ON_VECTOR = [0,1,0,0]
+RELU_ON_VECTOR = [0,0,1,0]
 STORES = [[0,1],[2],[3]]
 HELD = 2
 DMA_ALIGN = 256
@@ -34,6 +34,7 @@ def tile_picked_edgeup_relu_p_kernel(tc, x_words, x_scales, eT, w1, w2, w3, w4, 
     nc = tc.nc
     with ExitStack() as ctx:
         sb = ctx.enter_context(tc.tile_pool(name="sb", bufs=1))
+        reused = ctx.enter_context(tc.tile_pool(name="reused", bufs=1))
         ps = ctx.enter_context(tc.psum_pool(name="ps", bufs=1))
 
         def cast(on_vector, dst, src, as_activation=False):
@@ -50,8 +51,9 @@ def tile_picked_edgeup_relu_p_kernel(tc, x_words, x_scales, eT, w1, w2, w3, w4, 
             if share < whole:
                 cast(False, dst[:, share:whole], src[:, share:whole], as_activation)
 
-        def quantize(name, grouped, width, scales=None):
-            codes = sb.tile([P, width], U32, name=name + "_codes", align_bytes=64)
+        def quantize(name, grouped, width, scales=None, codes=None):
+            if codes is None:
+                codes = sb.tile([P, width], U32, name=name + "_codes", align_bytes=64)
             if scales is None:
                 scales = sb.tile([P, width], U8, name=name + "_scales", align_bytes=64)[:]
             nc.vector.quantize_mx(out=codes[:].bitcast(FP8X4), scales=scales, in_=grouped)
@@ -107,7 +109,9 @@ def tile_picked_edgeup_relu_p_kernel(tc, x_words, x_scales, eT, w1, w2, w3, w4, 
             nc.sync.dma_start(out=e_pairs[:, :, first:last], in_=e_rows[:, :, first:last])
         e_all = e_pairs[:].rearrange("p u (j c) -> p (u j) c", j=2)
         e_raw = [e_all[:, :, c * CHUNK : (c + 1) * CHUNK] for c in range(CHUNKS)]
-        (w4_raw,) = load_rows("w4_raw", w4)
+        w4_tile = reused.tile([P, PACK, N], F32, name="w4_raw", align_bytes=DMA_ALIGN, offset=0)
+        nc.sync.dma_start(out=w4_tile[:], in_=w4.rearrange("(p j) c -> p j c", j=PACK))
+        w4_raw = w4_tile[:]
 
         def round_first_weight(g, raw):
             grouped = sb.tile([P, PACK, P, PACK], BF16, name="w_grouped%d" % g, align_bytes=64)
@@ -179,7 +183,10 @@ def tile_picked_edgeup_relu_p_kernel(tc, x_words, x_scales, eT, w1, w2, w3, w4, 
             first_layer_pass(c, w3_q, e_codes, e_scales, False, True)
 
         def relu(c):
-            grouped = sb.tile([P, CHUNK, PACK], BF16, name="h_grouped%d" % c, tag="e3_grouped" if c == 1 else "h_grouped%d" % c, align_bytes=64)
+            if RELU_ON_VECTOR[c]:
+                grouped = reused.tile([P, CHUNK, PACK], BF16, name="h_grouped%d" % c, align_bytes=DMA_ALIGN, offset=0)
+            else:
+                grouped = sb.tile([P, CHUNK, PACK], BF16, name="h_grouped%d" % c, align_bytes=64)
             h_grouped[c] = grouped
             src = banks[c][:].rearrange("p t v -> p v t")
             if RELU_ON_VECTOR[c]:
@@ -188,7 +195,8 @@ def tile_picked_edgeup_relu_p_kernel(tc, x_words, x_scales, eT, w1, w2, w3, w4, 
                 nc.scalar.activation(out=grouped[:], in_=src, func=ACT.Relu)
 
         def second_layer(c, w4_q):
-            h_codes, h_scales = quantize("h%d" % c, h_grouped[c][:].rearrange("p v t -> p (v t)"), CHUNK)
+            codes = reused.tile([P, CHUNK], U32, name="h0_codes", align_bytes=DMA_ALIGN, offset=1024) if c == 0 else None
+            h_codes, h_scales = quantize("h%d" % c, h_grouped[c][:].rearrange("p v t -> p (v t)"), CHUNK, codes=codes)
             acc = ps.tile([P, CHUNK], F32, name="out_bank%d" % c)
             nc.tensor.matmul_mx(
                 out=acc[:],

@@ -26,7 +26,7 @@ W4_SHARE = 128
 RELU_ON_VECTOR = [0,0,1,0]
 STORES = [[0,1],[2],[3]]
 HELD = 2
-DMA_ALIGN = 256
+DMA_ALIGN = 1024
 OUT_ON_VECTOR = [0,0,0,0]
 
 
@@ -53,9 +53,9 @@ def tile_picked_edgeup_relu_p_kernel(tc, x_words, x_scales, eT, w1, w2, w3, w4, 
 
         def quantize(name, grouped, width, scales=None, codes=None):
             if codes is None:
-                codes = sb.tile([P, width], U32, name=name + "_codes", align_bytes=64)
+                codes = sb.tile([P, width], U32, name=name + "_codes", align_bytes=DMA_ALIGN)
             if scales is None:
-                scales = sb.tile([P, width], U8, name=name + "_scales", align_bytes=64)[:]
+                scales = sb.tile([P, width], U8, name=name + "_scales", align_bytes=DMA_ALIGN)[:]
             nc.vector.quantize_mx(out=codes[:].bitcast(FP8X4), scales=scales, in_=grouped)
             return codes[:], scales
 
@@ -114,21 +114,21 @@ def tile_picked_edgeup_relu_p_kernel(tc, x_words, x_scales, eT, w1, w2, w3, w4, 
         w4_raw = w4_tile[:]
 
         def round_first_weight(g, raw):
-            grouped = sb.tile([P, PACK, P, PACK], BF16, name="w_grouped%d" % g, align_bytes=64)
+            grouped = sb.tile([P, PACK, P, PACK], BF16, name="w_grouped%d" % g, align_bytes=DMA_ALIGN)
             dst = grouped[:].rearrange("p t m j -> p m j t")
             src = raw.rearrange("p j (m t) -> p m j t", t=PACK)
             shared_cast(dst, src, W_SHARE[g], P, g == 0)
             return grouped[:].rearrange("p t m j -> p (t m j)")
 
         def round_plain(name, raw, share):
-            grouped = sb.tile([P, CHUNK, PACK], BF16, name=name + "_grouped", tag=name + "_grouped", align_bytes=64)
+            grouped = sb.tile([P, CHUNK, PACK], BF16, name=name + "_grouped", tag=name + "_grouped", align_bytes=DMA_ALIGN)
             dst = grouped[:].rearrange("p (c i) j -> p c j i", i=4)
             src = raw.rearrange("p j (c i) -> p c j i", i=4)
             shared_cast(dst, src, share // 4, CHUNK // 4)
             return grouped[:].rearrange("p c j -> p (c j)")
 
         def gather_words(z, side):
-            picked = sb.tile([P, V], U32, name="x_picked%d%d" % (z, side), align_bytes=64)
+            picked = sb.tile([P, V], U32, name="x_picked%d%d" % (z, side), align_bytes=DMA_ALIGN)
             nc.vector.tensor_copy(picked[:], x_table[z].indirect(offsets[:, side * (V // 16) : (side + 1) * (V // 16)]))
             return picked
 
@@ -164,7 +164,7 @@ def tile_picked_edgeup_relu_p_kernel(tc, x_words, x_scales, eT, w1, w2, w3, w4, 
             tiles = column_tiles(quantize("w%d" % g, round_first_weight(g, node_passes[g][0]), H))
             for c in range(CHUNKS):
                 node_pass(g, tiles, c)
-        shared_scales = sb.tile([P, H], U8, name="shared_scales", align_bytes=64)
+        shared_scales = sb.tile([P, H], U8, name="shared_scales", align_bytes=DMA_ALIGN)
         last_tiles = column_tiles(quantize("w3", round_first_weight(3, node_passes[3][0]), H, shared_scales[:]))
         for c in range(CHUNKS - HELD):
             node_pass(3, last_tiles, c)
@@ -186,7 +186,7 @@ def tile_picked_edgeup_relu_p_kernel(tc, x_words, x_scales, eT, w1, w2, w3, w4, 
             if RELU_ON_VECTOR[c]:
                 grouped = reused.tile([P, CHUNK, PACK], BF16, name="h_grouped%d" % c, align_bytes=DMA_ALIGN, offset=0)
             else:
-                grouped = sb.tile([P, CHUNK, PACK], BF16, name="h_grouped%d" % c, align_bytes=64)
+                grouped = sb.tile([P, CHUNK, PACK], BF16, name="h_grouped%d" % c, align_bytes=DMA_ALIGN)
             h_grouped[c] = grouped
             src = banks[c][:].rearrange("p t v -> p v t")
             if RELU_ON_VECTOR[c]:

@@ -20,11 +20,11 @@ K_PASS = P * PACK
 CHUNK = 128
 CHUNKS = V // CHUNK
 E_LOADS = [[0],[1],[2],[3]]
-W_SHARE = [0,48,64,64,80]
+W_SHARE = [0,0,64,64,80]
 E_SHARE = [0,128,0,128]
 W4_SHARE = 128
 RELU_ON_VECTOR = [0,0,1,0]
-STORES = [[0,1],[2],[3]]
+STORES = [[0],[1],[2],[3]]
 HELD = 2
 DMA_ALIGN = 1024
 OUT_ON_VECTOR = [0,0,0,0]
@@ -62,9 +62,7 @@ def tile_picked_edgeup_relu_p_kernel(tc, x_words, x_scales, eT, w1, w2, w3, w4, 
         offsets = sb.tile([P, S // 16], U16, name="offsets", align_bytes=DMA_ALIGN)
         scale_rows = sb.tile([P, T], U8, name="scale_rows", align_bytes=DMA_ALIGN)
         x_picked_plane = sb.tile([P, S], U8, name="x_picked_plane", align_bytes=DMA_ALIGN)
-        nc.gpsimd.memset(scale_rows[32:64, :].bitcast(I32), 0)
-        nc.gpsimd.memset(scale_rows[64:P, :].bitcast(I32), 0)
-        nc.gpsimd.memset(x_picked_plane[:].bitcast(I32), 0)
+        nc.gpsimd.memset(scale_rows[:].bitcast(I32), 0)
 
         def load_rows(name, rows):
             passes = rows.shape[0] // K_PASS
@@ -72,31 +70,28 @@ def tile_picked_edgeup_relu_p_kernel(tc, x_words, x_scales, eT, w1, w2, w3, w4, 
             nc.sync.dma_start(out=raw[:], in_=rows.rearrange("(z p j) c -> p z j c", j=PACK, p=P))
             return [raw[:, z] for z in range(passes)]
 
-        def load_x():
-            table = sb.tile([P, 2, T], U32, name="x_table", align_bytes=DMA_ALIGN)
-            nc.sync.dma_start(
-                out=table[:].bitcast(I32),
-                in_=x_words.rearrange("z p c r -> p z (c r)").bitcast(I32),
-            )
-            return [table[:, z, :] for z in range(2)]
+        def load_x(z):
+            table = sb.tile([P, T], U32, name="x_table%d" % z, align_bytes=DMA_ALIGN)
+            nc.sync.dma_start(out=table[:].bitcast(I32), in_=x_words[z].rearrange("p c r -> p (c r)").bitcast(I32))
+            return table[:]
 
-        def place_scale_rows(rows):
-            for r in rows:
-                for z in range(2):
-                    nc.sync.dma_start(
-                        out=x_picked_plane[4 * z + r : P : 32, :].bitcast(I32),
-                        in_=picked_rows[16 * z + r : 16 * (z + 1) : 4, :].bitcast(I32),
-                    )
+        def place_scale_rows(z):
+            for r in range(1, 4):
+                nc.sync.dma_start(
+                    out=x_picked_plane[4 * z + r : P : 32, :].bitcast(I32),
+                    in_=picked_rows[4 * z + 8 * r : P : 32, :].bitcast(I32),
+                )
 
-        nc.sync.dma_start(out=scale_rows[0:32, :].bitcast(I32), in_=x_scales.rearrange("z q c -> (z q) c").bitcast(I32))
+        (w1a,) = load_rows("w1a", w1[0:K_PASS, :])
+        nc.sync.dma_start(out=scale_rows[0:P:4, :].bitcast(I32), in_=x_scales.rearrange("z q c -> q z c").bitcast(I32))
         nc.sync.dma_start(offsets[:], offs)
         picked_rows = sb.tile([P, S], U8, name="picked_rows", align_bytes=DMA_ALIGN)
         nc.vector.tensor_copy(picked_rows[:], scale_rows[:].indirect(offsets[:]))
-        x_table = load_x()
-        (w1a,) = load_rows("w1a", w1[0:K_PASS, :])
-        place_scale_rows((0, 1))
+        nc.vector.tensor_copy(x_picked_plane[:].bitcast(I32), picked_rows[:].bitcast(I32))
+        x_table = [load_x(z) for z in range(2)]
         (w2a,) = load_rows("w2a", w2[0:K_PASS, :])
-        place_scale_rows((2, 3))
+        place_scale_rows(0)
+        place_scale_rows(1)
         (w1b,) = load_rows("w1b", w1[K_PASS:K, :])
         (w2b,) = load_rows("w2b", w2[K_PASS:K, :])
         node_passes = [(w1a, 0, 0), (w2a, 0, 1), (w1b, 1, 0), (w2b, 1, 1)]

@@ -17,17 +17,18 @@ ACT = mybir.ActivationFunctionType
 P = 128
 PACK = 4
 K_PASS = P * PACK
+QUADRANT = 32
+PLANE_STEP = 4
 CHUNK = 128
 CHUNKS = V // CHUNK
-E_LOADS = [[0],[1],[2],[3]]
-W_SHARE = [0,0,64,64,80]
-E_SHARE = [0,128,0,128]
-W4_SHARE = 128
-RELU_ON_VECTOR = [0,0,1,0]
-STORES = [[0],[1],[2],[3]]
+RUN = 4
+
+ALIGN = 256
+
+NODE_SHARES = [0, 0, 48, 64]
+W3_SHARE = 80
 HELD = 2
-DMA_ALIGN = 1024
-OUT_ON_VECTOR = [0,0,0,0]
+VECTOR_RELU = 2
 
 
 def tile_picked_edgeup_relu_p_kernel(tc, x_words, x_scales, eT, w1, w2, w3, w4, offs, out):
@@ -37,183 +38,145 @@ def tile_picked_edgeup_relu_p_kernel(tc, x_words, x_scales, eT, w1, w2, w3, w4, 
         reused = ctx.enter_context(tc.tile_pool(name="reused", bufs=1))
         ps = ctx.enter_context(tc.psum_pool(name="ps", bufs=1))
 
-        def cast(on_vector, dst, src, as_activation=False):
-            if on_vector:
-                nc.vector.tensor_copy(out=dst, in_=src)
-            elif as_activation:
-                nc.scalar.activation(out=dst, in_=src, func=ACT.Copy)
-            else:
-                nc.scalar.copy(out=dst, in_=src)
-
-        def shared_cast(dst, src, share, whole, as_activation=False):
+        def round_shared(dst, src, share):
             if share > 0:
-                cast(True, dst[:, 0:share], src[:, 0:share])
-            if share < whole:
-                cast(False, dst[:, share:whole], src[:, share:whole], as_activation)
+                nc.vector.tensor_copy(out=dst[:, :share], in_=src[:, :share])
+            if share < dst.shape[1]:
+                nc.scalar.activation(out=dst[:, share:], in_=src[:, share:], func=ACT.Copy)
 
-        def quantize(name, grouped, width, scales=None, codes=None):
+        def quantize(name, grouped, codes=None, scales=None):
+            width = grouped.shape[1] // PACK
             if codes is None:
-                codes = sb.tile([P, width], U32, name=name + "_codes", align_bytes=DMA_ALIGN)
+                codes = sb.tile([P, width], U32, name=name + "_codes", align_bytes=ALIGN)[:]
             if scales is None:
-                scales = sb.tile([P, width], U8, name=name + "_scales", align_bytes=DMA_ALIGN)[:]
-            nc.vector.quantize_mx(out=codes[:].bitcast(FP8X4), scales=scales, in_=grouped)
-            return codes[:], scales
+                scales = sb.tile([P, width], U8, name=name + "_scales", align_bytes=ALIGN)[:]
+            nc.vector.quantize_mx(out=codes.bitcast(FP8X4), scales=scales, in_=grouped)
+            return [(codes[:, first : first + P], scales[:, first : first + P]) for first in range(0, width, P)]
 
-        offsets = sb.tile([P, S // 16], U16, name="offsets", align_bytes=DMA_ALIGN)
-        scale_rows = sb.tile([P, T], U8, name="scale_rows", align_bytes=DMA_ALIGN)
-        x_picked_plane = sb.tile([P, S], U8, name="x_picked_plane", align_bytes=DMA_ALIGN)
-        nc.gpsimd.memset(scale_rows[:].bitcast(I32), 0)
+        def mx_pass(acc, stationary, moving, start, stop):
+            nc.tensor.matmul_mx(
+                out=acc,
+                lhsT=stationary[0].bitcast(FP8X4),
+                lhsT_scale=stationary[1],
+                rhs=moving[0].bitcast(FP8X4),
+                rhs_scale=moving[1],
+                start=start,
+                stop=stop,
+            )
 
-        def load_rows(name, rows):
-            passes = rows.shape[0] // K_PASS
-            raw = sb.tile([P, passes, PACK, rows.shape[1]], F32, name=name, align_bytes=DMA_ALIGN)
-            nc.sync.dma_start(out=raw[:], in_=rows.rearrange("(z p j) c -> p z j c", j=PACK, p=P))
-            return [raw[:, z] for z in range(passes)]
+        def load_weight(name, rows):
+            raw = sb.tile([P, PACK, H], F32, name=name, align_bytes=ALIGN)
+            nc.sync.dma_start(out=raw[:], in_=rows.rearrange("(p j) c -> p j c", j=PACK))
+            return raw[:].rearrange("p j (m t) -> p m j t", t=PACK)
 
-        def load_x(z):
-            table = sb.tile([P, T], U32, name="x_table%d" % z, align_bytes=DMA_ALIGN)
+        def load_table(z):
+            table = sb.tile([P, T], U32, name="x_table%d" % z, align_bytes=ALIGN)
             nc.sync.dma_start(out=table[:].bitcast(I32), in_=x_words[z].rearrange("p c r -> p (c r)").bitcast(I32))
             return table[:]
 
-        def place_scale_rows(z):
+        offsets = sb.tile([P, S // 16], U16, name="offsets", align_bytes=ALIGN)
+        scale_rows = sb.tile([P, T], U8, name="scale_rows", align_bytes=ALIGN)
+        nc.gpsimd.memset(scale_rows[:].bitcast(I32), 0)
+        w1a = load_weight("w1a", w1[0:K_PASS, :])
+        nc.sync.dma_start(out=scale_rows[0:P:PLANE_STEP, :].bitcast(I32), in_=x_scales.rearrange("z b c -> b z c").bitcast(I32))
+        nc.sync.dma_start(offsets[:], offs)
+
+        picked_rows = sb.tile([P, S], U8, name="picked_rows", align_bytes=ALIGN)
+        x_planes = sb.tile([P, S], U8, name="x_planes", align_bytes=ALIGN)
+        nc.vector.tensor_copy(picked_rows[:], scale_rows[:].indirect(offsets[:]))
+        nc.vector.tensor_copy(x_planes[:].bitcast(I32), picked_rows[:].bitcast(I32))
+        x_tables = [load_table(0)]
+        w2a = load_weight("w2a", w2[0:K_PASS, :])
+        x_tables.append(load_table(1))
+        for z in range(2):
             for r in range(1, 4):
                 nc.sync.dma_start(
-                    out=x_picked_plane[4 * z + r : P : 32, :].bitcast(I32),
-                    in_=picked_rows[4 * z + 8 * r : P : 32, :].bitcast(I32),
+                    out=x_planes[PLANE_STEP * z + r : P : QUADRANT, :].bitcast(I32),
+                    in_=picked_rows[PLANE_STEP * z + 8 * r : P : QUADRANT, :].bitcast(I32),
                 )
-
-        (w1a,) = load_rows("w1a", w1[0:K_PASS, :])
-        nc.sync.dma_start(out=scale_rows[0:P:4, :].bitcast(I32), in_=x_scales.rearrange("z q c -> q z c").bitcast(I32))
-        nc.sync.dma_start(offsets[:], offs)
-        picked_rows = sb.tile([P, S], U8, name="picked_rows", align_bytes=DMA_ALIGN)
-        nc.vector.tensor_copy(picked_rows[:], scale_rows[:].indirect(offsets[:]))
-        nc.vector.tensor_copy(x_picked_plane[:].bitcast(I32), picked_rows[:].bitcast(I32))
-        x_table = [load_x(z) for z in range(2)]
-        (w2a,) = load_rows("w2a", w2[0:K_PASS, :])
-        place_scale_rows(0)
-        place_scale_rows(1)
-        (w1b,) = load_rows("w1b", w1[K_PASS:K, :])
-        (w2b,) = load_rows("w2b", w2[K_PASS:K, :])
+        w1b = load_weight("w1b", w1[K_PASS:K, :])
+        w2b = load_weight("w2b", w2[K_PASS:K, :])
         node_passes = [(w1a, 0, 0), (w2a, 0, 1), (w1b, 1, 0), (w2b, 1, 1)]
-        (w3_raw,) = load_rows("w3_raw", w3)
-        e_pairs = sb.tile([P, 2, 2 * V], F32, name="e_pairs", align_bytes=DMA_ALIGN)
+        w3_raw = load_weight("w3_raw", w3)
+
+        e_pairs = sb.tile([P, 2, 2 * V], F32, name="e_pairs", align_bytes=ALIGN)
         e_rows = eT.rearrange("(p u j) c -> p u (j c)", u=2, j=2)
-        for chunks in E_LOADS:
-            first = V + chunks[0] * CHUNK if chunks[0] > 0 else 0
-            last = V + (chunks[-1] + 1) * CHUNK
+        cuts = [0] + [V + (c + 1) * CHUNK for c in range(CHUNKS)]
+        for first, last in zip(cuts, cuts[1:]):
             nc.sync.dma_start(out=e_pairs[:, :, first:last], in_=e_rows[:, :, first:last])
-        e_all = e_pairs[:].rearrange("p u (j c) -> p (u j) c", j=2)
-        e_raw = [e_all[:, :, c * CHUNK : (c + 1) * CHUNK] for c in range(CHUNKS)]
-        w4_tile = reused.tile([P, PACK, N], F32, name="w4_raw", align_bytes=DMA_ALIGN, offset=0)
-        nc.sync.dma_start(out=w4_tile[:], in_=w4.rearrange("(p j) c -> p j c", j=PACK))
-        w4_raw = w4_tile[:]
-
-        def round_first_weight(g, raw):
-            grouped = sb.tile([P, PACK, P, PACK], BF16, name="w_grouped%d" % g, align_bytes=DMA_ALIGN)
-            dst = grouped[:].rearrange("p t m j -> p m j t")
-            src = raw.rearrange("p j (m t) -> p m j t", t=PACK)
-            shared_cast(dst, src, W_SHARE[g], P, g == 0)
-            return grouped[:].rearrange("p t m j -> p (t m j)")
-
-        def round_plain(name, raw, share):
-            grouped = sb.tile([P, CHUNK, PACK], BF16, name=name + "_grouped", tag=name + "_grouped", align_bytes=DMA_ALIGN)
-            dst = grouped[:].rearrange("p (c i) j -> p c j i", i=4)
-            src = raw.rearrange("p j (c i) -> p c j i", i=4)
-            shared_cast(dst, src, share // 4, CHUNK // 4)
-            return grouped[:].rearrange("p c j -> p (c j)")
+        e_raw = e_pairs[:].rearrange("p u (j c) -> p (u j) c", j=2)
+        w4_raw = reused.tile([P, PACK, N], F32, name="w4_raw", align_bytes=ALIGN, offset=0)
+        nc.sync.dma_start(out=w4_raw[:], in_=w4.rearrange("(p j) c -> p j c", j=PACK))
 
         def gather_words(z, side):
-            picked = sb.tile([P, V], U32, name="x_picked%d%d" % (z, side), align_bytes=DMA_ALIGN)
-            nc.vector.tensor_copy(picked[:], x_table[z].indirect(offsets[:, side * (V // 16) : (side + 1) * (V // 16)]))
+            picked = sb.tile([P, V], U32, name="x_picked%d%d" % (z, side), align_bytes=ALIGN)
+            nc.vector.tensor_copy(picked[:], x_tables[z].indirect(offsets[:, side * (V // 16) : (side + 1) * (V // 16)]))
             return picked
 
         x_picked = [[gather_words(z, side) for side in range(2)] for z in range(2)]
-
         banks = [ps.tile([P, PACK, CHUNK], F32, name="h_bank%d" % c) for c in range(CHUNKS)]
 
-        def column_tiles(w):
-            codes, scales = w
-            return [(codes[:, first : first + P], scales[:, first : first + P]) for first in range(0, codes.shape[1], P)]
+        def round_weight(name, raw, share):
+            grouped = sb.tile([P, PACK, P, PACK], BF16, name=name, align_bytes=ALIGN)
+            round_shared(grouped[:].rearrange("p t m j -> p m j t"), raw, share)
+            return grouped[:].rearrange("p t m j -> p (t m j)")
 
-        def first_layer_pass(c, tiles, rhs, rhs_scale, first, last):
-            for t, (codes, scales) in enumerate(tiles):
-                nc.tensor.matmul_mx(
-                    out=banks[c][:, t, :],
-                    lhsT=codes.bitcast(FP8X4),
-                    lhsT_scale=scales,
-                    rhs=rhs.bitcast(FP8X4),
-                    rhs_scale=rhs_scale,
-                    start=(first and t == 0),
-                    stop=(last and t == PACK - 1),
-                )
+        def round_columns(name, raw, share):
+            grouped = sb.tile([P, CHUNK, PACK], BF16, name=name, align_bytes=ALIGN)
+            dst = grouped[:].rearrange("p (c i) j -> p c j i", i=RUN)
+            round_shared(dst, raw.rearrange("p j (c i) -> p c j i", i=RUN), share // RUN)
+            return grouped[:].rearrange("p c j -> p (c j)")
 
-        def node_pass(g, tiles, c):
+        def first_layer_pass(c, tiles, moving, opens, closes):
+            for t, stationary in enumerate(tiles):
+                mx_pass(banks[c][:, t, :], stationary, moving, opens and t == 0, closes and t == PACK - 1)
+
+        def node_pass(g, tiles, chunks):
             z, side = node_passes[g][1:]
-            first_layer_pass(
-                c, tiles, x_picked[z][side][:, c * CHUNK : (c + 1) * CHUNK],
-                x_picked_plane[4 * z : P, side * V + c * CHUNK : side * V + (c + 1) * CHUNK],
-                g == 0, False,
-            )
+            for c in chunks:
+                words = x_picked[z][side][:, c * CHUNK : (c + 1) * CHUNK]
+                scales = x_planes[PLANE_STEP * z : P, side * V + c * CHUNK : side * V + (c + 1) * CHUNK]
+                first_layer_pass(c, tiles, (words, scales), g == 0, False)
 
-        for g in range(3):
-            tiles = column_tiles(quantize("w%d" % g, round_first_weight(g, node_passes[g][0]), H))
-            for c in range(CHUNKS):
-                node_pass(g, tiles, c)
-        shared_scales = sb.tile([P, H], U8, name="shared_scales", align_bytes=DMA_ALIGN)
-        last_tiles = column_tiles(quantize("w3", round_first_weight(3, node_passes[3][0]), H, shared_scales[:]))
-        for c in range(CHUNKS - HELD):
-            node_pass(3, last_tiles, c)
-        w3_grouped = round_first_weight(4, w3_raw)
+        last = len(node_passes) - 1
+        for g in range(last):
+            grouped = round_weight("w_grouped%d" % g, node_passes[g][0], NODE_SHARES[g])
+            node_pass(g, quantize("w%d" % g, grouped), range(CHUNKS))
+
+        shared_scales = sb.tile([P, H], U8, name="shared_scales", align_bytes=ALIGN)
+        grouped = round_weight("w_grouped%d" % last, node_passes[last][0], NODE_SHARES[last])
+        last_tiles = quantize("w%d" % last, grouped, scales=shared_scales[:])
+        node_pass(last, last_tiles, range(CHUNKS - HELD))
+        w3_grouped = round_weight("w3_grouped", w3_raw, W3_SHARE)
         half = H // 2
-        w3_q = column_tiles(quantize("w4a", w3_grouped[:, 0 : PACK * half], half, shared_scales[4:P, 0:half]))
-        for c in range(CHUNKS - HELD, CHUNKS):
-            node_pass(3, last_tiles, c)
-        w3_q = w3_q + column_tiles(quantize("w4b", w3_grouped[:, PACK * half : PACK * H], half))
+        w3_tiles = quantize("w3a", w3_grouped[:, 0 : PACK * half], scales=shared_scales[PLANE_STEP:P, 0:half])
+        node_pass(last, last_tiles, range(CHUNKS - HELD, CHUNKS))
+        w3_tiles = w3_tiles + quantize("w3b", w3_grouped[:, PACK * half : PACK * H])
 
-        h_grouped = {}
-        results = {}
-
-        def edge_pass(c):
-            e_codes, e_scales = quantize("e%d" % c, round_plain("e%d" % c, e_raw[c], E_SHARE[c]), CHUNK)
-            first_layer_pass(c, w3_q, e_codes, e_scales, False, True)
+        for c in range(CHUNKS):
+            grouped = round_columns("e_grouped%d" % c, e_raw[:, :, c * CHUNK : (c + 1) * CHUNK], CHUNK * (c % 2))
+            (e_q,) = quantize("e%d" % c, grouped)
+            first_layer_pass(c, w3_tiles, e_q, False, True)
+        (w4_q,) = quantize("w4", round_columns("w4_grouped", w4_raw[:], N))
 
         def relu(c):
-            if RELU_ON_VECTOR[c]:
-                grouped = reused.tile([P, CHUNK, PACK], BF16, name="h_grouped%d" % c, align_bytes=DMA_ALIGN, offset=0)
-            else:
-                grouped = sb.tile([P, CHUNK, PACK], BF16, name="h_grouped%d" % c, align_bytes=DMA_ALIGN)
-            h_grouped[c] = grouped
             src = banks[c][:].rearrange("p t v -> p v t")
-            if RELU_ON_VECTOR[c]:
+            if c == VECTOR_RELU:
+                grouped = reused.tile([P, CHUNK, PACK], BF16, name="h_grouped%d" % c, align_bytes=ALIGN, offset=0)
                 nc.vector.tensor_scalar_max(out=grouped[:], in0=src, scalar1=0.0)
             else:
+                grouped = sb.tile([P, CHUNK, PACK], BF16, name="h_grouped%d" % c, align_bytes=ALIGN)
                 nc.scalar.activation(out=grouped[:], in_=src, func=ACT.Relu)
+            return grouped[:].rearrange("p v t -> p (v t)")
 
-        def second_layer(c, w4_q):
-            codes = reused.tile([P, CHUNK], U32, name="h0_codes", align_bytes=DMA_ALIGN, offset=1024) if c == 0 else None
-            h_codes, h_scales = quantize("h%d" % c, h_grouped[c][:].rearrange("p v t -> p (v t)"), CHUNK, codes=codes)
+        h_grouped = [relu(c) for c in range(CHUNKS)]
+        h_bytes = CHUNK * PACK * 2
+        h0_codes = reused.tile([P, CHUNK], U32, name="h0_codes", align_bytes=ALIGN, offset=h_bytes)
+
+        for c in range(CHUNKS):
+            (h_q,) = quantize("h%d" % c, h_grouped[c], codes=h0_codes[:] if c == 0 else None)
             acc = ps.tile([P, CHUNK], F32, name="out_bank%d" % c)
-            nc.tensor.matmul_mx(
-                out=acc[:],
-                lhsT=w4_q[0].bitcast(FP8X4),
-                lhsT_scale=w4_q[1],
-                rhs=h_codes.bitcast(FP8X4),
-                rhs_scale=h_scales,
-                start=True,
-                stop=True,
-            )
-            (group,) = [chunks for chunks in STORES if c in chunks]
-            if c == group[0]:
-                results[c] = sb.tile([P, len(group) * CHUNK], F32, name="result%d" % c, align_bytes=DMA_ALIGN)
-            result = results[group[0]]
-            cast(OUT_ON_VECTOR[c], result[:, (c - group[0]) * CHUNK : (c - group[0] + 1) * CHUNK], acc[:])
-            if c == group[-1]:
-                nc.sync.dma_start(out=out[:, group[0] * CHUNK : (c + 1) * CHUNK], in_=result[:])
-
-        for c in range(CHUNKS):
-            edge_pass(c)
-        w4_q = quantize("w4", round_plain("w4", w4_raw, W4_SHARE), CHUNK)
-        for c in range(CHUNKS):
-            relu(c)
-        for c in range(CHUNKS):
-            second_layer(c, w4_q)
+            mx_pass(acc[:], w4_q, h_q, True, True)
+            result = sb.tile([P, CHUNK], F32, name="result%d" % c, align_bytes=ALIGN)
+            nc.scalar.activation(out=result[:], in_=acc[:], func=ACT.Copy)
+            nc.sync.dma_start(out=out[:, c * CHUNK : (c + 1) * CHUNK], in_=result[:])

@@ -65,9 +65,9 @@ def tile_picked_edgeup_relu_p_kernel(tc, x_words, x_scales, eT, w1, w2, w3, w4, 
             )
 
         def load_weight(name, rows):
-            raw = sb.tile([P, PACK, H], F32, name=name, align_bytes=ALIGN)
-            nc.sync.dma_start(out=raw[:], in_=rows.rearrange("(p j) c -> p j c", j=PACK))
-            return raw[:].rearrange("p j (m t) -> p m j t", t=PACK)
+            raw = sb.tile([P, PACK * H], F32, name=name, align_bytes=ALIGN)
+            nc.sync.dma_start(out=raw[:], in_=rows.rearrange("(p j) c -> p (j c)", j=PACK))
+            return raw[:].rearrange("p (j m t) -> p m j t", j=PACK, t=PACK)
 
         def load_table(z):
             table = sb.tile([P, T], U32, name="x_table%d" % z, align_bytes=ALIGN)
@@ -76,7 +76,7 @@ def tile_picked_edgeup_relu_p_kernel(tc, x_words, x_scales, eT, w1, w2, w3, w4, 
 
         offsets = sb.tile([P, S // 16], U16, name="offsets", align_bytes=ALIGN)
         scale_rows = sb.tile([P, T], U8, name="scale_rows", align_bytes=ALIGN)
-        nc.gpsimd.memset(scale_rows[:].bitcast(I32), 0)
+        nc.vector.memset(scale_rows[:].bitcast(I32), 0)
         w1a = load_weight("w1a", w1[0:K_PASS, :])
         nc.sync.dma_start(out=scale_rows[0:P:PLANE_STEP, :].bitcast(I32), in_=x_scales.rearrange("z b c -> b z c").bitcast(I32))
         nc.sync.dma_start(offsets[:], offs)
@@ -105,8 +105,8 @@ def tile_picked_edgeup_relu_p_kernel(tc, x_words, x_scales, eT, w1, w2, w3, w4, 
         for first, last in zip(cuts, cuts[1:]):
             nc.sync.dma_start(out=e_pairs[:, :, first:last], in_=e_rows[:, :, first:last])
         e_raw = e_pairs[:].rearrange("p u (j c) -> p (u j) c", j=2)
-        w4_raw = reused.tile([P, PACK, N], F32, name="w4_raw", align_bytes=ALIGN, offset=0)
-        nc.sync.dma_start(out=w4_raw[:], in_=w4.rearrange("(p j) c -> p j c", j=PACK))
+        w4_raw = reused.tile([P, PACK * N], F32, name="w4_raw", align_bytes=ALIGN, offset=0)
+        nc.sync.dma_start(out=w4_raw[:], in_=w4.rearrange("(p j) c -> p (j c)", j=PACK))
 
         def gather_words(z, side):
             picked = sb.tile([P, V], U32, name="x_picked%d%d" % (z, side), align_bytes=ALIGN)
@@ -157,7 +157,7 @@ def tile_picked_edgeup_relu_p_kernel(tc, x_words, x_scales, eT, w1, w2, w3, w4, 
             grouped = round_columns("e_grouped%d" % c, e_raw[:, :, c * CHUNK : (c + 1) * CHUNK], CHUNK * (c % 2))
             (e_q,) = quantize("e%d" % c, grouped)
             first_layer_pass(c, w3_tiles, e_q, False, True)
-        (w4_q,) = quantize("w4", round_columns("w4_grouped", w4_raw[:], N))
+        (w4_q,) = quantize("w4", round_columns("w4_grouped", w4_raw[:].rearrange("p (j c) -> p j c", j=PACK), N))
 
         def relu(c):
             src = banks[c][:].rearrange("p t v -> p v t")

from contextlib import ExitStack

import concourse.mybir as mybir

K, T, S, V, H, N, J = 1024, 2048, 1024, 512, 512, 128, 512
FLOPS = 2 * (2 * K + J) * H * V + 2 * H * N * V

F32 = mybir.dt.float32
BF16 = mybir.dt.bfloat16
I32 = mybir.dt.int32
U32 = mybir.dt.uint32
U16 = mybir.dt.uint16
U8 = mybir.dt.uint8
FP8X4 = mybir.dt.float8_e4m3fn_x4
ACT = mybir.ActivationFunctionType

P = 128
PACK = 4
K_PASS = P * PACK
QUADRANT = 32
PLANE_STEP = 4
CHUNK = 128
CHUNKS = V // CHUNK
RUN = 4

ALIGN = 256

NODE_SHARES = [0, 0, 48, 64]
W3_SHARE = 80
HELD = 2
VECTOR_RELU = 2


def tile_picked_edgeup_relu_p_kernel(tc, x_words, x_scales, eT, w1, w2, w3, w4, offs, out):
    nc = tc.nc
    with ExitStack() as ctx:
        sb = ctx.enter_context(tc.tile_pool(name="sb", bufs=1))
        reused = ctx.enter_context(tc.tile_pool(name="reused", bufs=1))
        ps = ctx.enter_context(tc.psum_pool(name="ps", bufs=1))

        def round_shared(dst, src, share):
            if share > 0:
                nc.vector.tensor_copy(out=dst[:, :share], in_=src[:, :share])
            if share < dst.shape[1]:
                nc.scalar.activation(out=dst[:, share:], in_=src[:, share:], func=ACT.Copy)

        def quantize(name, grouped, codes=None, scales=None):
            width = grouped.shape[1] // PACK
            if codes is None:
                codes = sb.tile([P, width], U32, name=name + "_codes", align_bytes=ALIGN)[:]
            if scales is None:
                scales = sb.tile([P, width], U8, name=name + "_scales", align_bytes=ALIGN)[:]
            nc.vector.quantize_mx(out=codes.bitcast(FP8X4), scales=scales, in_=grouped)
            return [(codes[:, first : first + P], scales[:, first : first + P]) for first in range(0, width, P)]

        def mx_pass(acc, stationary, moving, start, stop):
            nc.tensor.matmul_mx(
                out=acc,
                lhsT=stationary[0].bitcast(FP8X4),
                lhsT_scale=stationary[1],
                rhs=moving[0].bitcast(FP8X4),
                rhs_scale=moving[1],
                start=start,
                stop=stop,
            )

        def load_weight(name, rows):
            raw = sb.tile([P, PACK * H], F32, name=name, align_bytes=ALIGN)
            nc.sync.dma_start(out=raw[:], in_=rows.rearrange("(p j) c -> p (j c)", j=PACK))
            return raw[:].rearrange("p (j m t) -> p m j t", j=PACK, t=PACK)

        def load_table(z):
            table = sb.tile([P, T], U32, name="x_table%d" % z, align_bytes=ALIGN)
            nc.sync.dma_start(out=table[:].bitcast(I32), in_=x_words[z].rearrange("p c r -> p (c r)").bitcast(I32))
            return table[:]

        offsets = sb.tile([P, S // 16], U16, name="offsets", align_bytes=ALIGN)
        scale_rows = sb.tile([P, T], U8, name="scale_rows", align_bytes=ALIGN)
        nc.vector.memset(scale_rows[:].bitcast(I32), 0)
        w1a = load_weight("w1a", w1[0:K_PASS, :])
        nc.sync.dma_start(out=scale_rows[0:P:PLANE_STEP, :].bitcast(I32), in_=x_scales.rearrange("z b c -> b z c").bitcast(I32))
        nc.sync.dma_start(offsets[:], offs)

        picked_rows = sb.tile([P, S], U8, name="picked_rows", align_bytes=ALIGN)
        x_planes = sb.tile([P, S], U8, name="x_planes", align_bytes=ALIGN)
        nc.vector.tensor_copy(picked_rows[:], scale_rows[:].indirect(offsets[:]))
        nc.vector.tensor_copy(x_planes[:].bitcast(I32), picked_rows[:].bitcast(I32))
        x_tables = [load_table(0)]
        w2a = load_weight("w2a", w2[0:K_PASS, :])
        x_tables.append(load_table(1))
        for z in range(2):
            for r in range(1, 4):
                nc.sync.dma_start(
                    out=x_planes[PLANE_STEP * z + r : P : QUADRANT, :].bitcast(I32),
                    in_=picked_rows[PLANE_STEP * z + 8 * r : P : QUADRANT, :].bitcast(I32),
                )
        w1b = load_weight("w1b", w1[K_PASS:K, :])
        w2b = load_weight("w2b", w2[K_PASS:K, :])
        node_passes = [(w1a, 0, 0), (w2a, 0, 1), (w1b, 1, 0), (w2b, 1, 1)]
        w3_raw = load_weight("w3_raw", w3)

        e_pairs = sb.tile([P, 2, 2 * V], F32, name="e_pairs", align_bytes=ALIGN)
        e_rows = eT.rearrange("(p u j) c -> p u (j c)", u=2, j=2)
        cuts = [0] + [V + (c + 1) * CHUNK for c in range(CHUNKS)]
        for first, last in zip(cuts, cuts[1:]):
            nc.sync.dma_start(out=e_pairs[:, :, first:last], in_=e_rows[:, :, first:last])
        e_raw = e_pairs[:].rearrange("p u (j c) -> p (u j) c", j=2)
        w4_raw = reused.tile([P, PACK * N], F32, name="w4_raw", align_bytes=ALIGN, offset=0)
        nc.sync.dma_start(out=w4_raw[:], in_=w4.rearrange("(p j) c -> p (j c)", j=PACK))

        def gather_words(z, side):
            picked = sb.tile([P, V], U32, name="x_picked%d%d" % (z, side), align_bytes=ALIGN)
            nc.vector.tensor_copy(picked[:], x_tables[z].indirect(offsets[:, side * (V // 16) : (side + 1) * (V // 16)]))
            return picked

        x_picked = [[gather_words(z, side) for side in range(2)] for z in range(2)]
        banks = [ps.tile([P, PACK, CHUNK], F32, name="h_bank%d" % c) for c in range(CHUNKS)]

        def round_weight(name, raw, share):
            grouped = sb.tile([P, PACK, P, PACK], BF16, name=name, align_bytes=ALIGN)
            round_shared(grouped[:].rearrange("p t m j -> p m j t"), raw, share)
            return grouped[:].rearrange("p t m j -> p (t m j)")

        def round_columns(name, raw, share):
            grouped = sb.tile([P, CHUNK, PACK], BF16, name=name, align_bytes=ALIGN)
            dst = grouped[:].rearrange("p (c i) j -> p c j i", i=RUN)
            round_shared(dst, raw.rearrange("p j (c i) -> p c j i", i=RUN), share // RUN)
            return grouped[:].rearrange("p c j -> p (c j)")

        def first_layer_pass(c, tiles, moving, opens, closes):
            for t, stationary in enumerate(tiles):
                mx_pass(banks[c][:, t, :], stationary, moving, opens and t == 0, closes and t == PACK - 1)

        def node_pass(g, tiles, chunks):
            z, side = node_passes[g][1:]
            for c in chunks:
                words = x_picked[z][side][:, c * CHUNK : (c + 1) * CHUNK]
                scales = x_planes[PLANE_STEP * z : P, side * V + c * CHUNK : side * V + (c + 1) * CHUNK]
                first_layer_pass(c, tiles, (words, scales), g == 0, False)

        last = len(node_passes) - 1
        for g in range(last):
            grouped = round_weight("w_grouped%d" % g, node_passes[g][0], NODE_SHARES[g])
            node_pass(g, quantize("w%d" % g, grouped), range(CHUNKS))

        shared_scales = sb.tile([P, H], U8, name="shared_scales", align_bytes=ALIGN)
        grouped = round_weight("w_grouped%d" % last, node_passes[last][0], NODE_SHARES[last])
        last_tiles = quantize("w%d" % last, grouped, scales=shared_scales[:])
        node_pass(last, last_tiles, range(CHUNKS - HELD))
        w3_grouped = round_weight("w3_grouped", w3_raw, W3_SHARE)
        half = H // 2
        w3_tiles = quantize("w3a", w3_grouped[:, 0 : PACK * half], scales=shared_scales[PLANE_STEP:P, 0:half])
        node_pass(last, last_tiles, range(CHUNKS - HELD, CHUNKS))
        w3_tiles = w3_tiles + quantize("w3b", w3_grouped[:, PACK * half : PACK * H])

        for c in range(CHUNKS):
            grouped = round_columns("e_grouped%d" % c, e_raw[:, :, c * CHUNK : (c + 1) * CHUNK], CHUNK * (c % 2))
            (e_q,) = quantize("e%d" % c, grouped)
            first_layer_pass(c, w3_tiles, e_q, False, True)
        (w4_q,) = quantize("w4", round_columns("w4_grouped", w4_raw[:].rearrange("p (j c) -> p j c", j=PACK), N))

        def relu(c):
            src = banks[c][:].rearrange("p t v -> p v t")
            if c == VECTOR_RELU:
                grouped = reused.tile([P, CHUNK, PACK], BF16, name="h_grouped%d" % c, align_bytes=ALIGN, offset=0)
                nc.vector.tensor_scalar_max(out=grouped[:], in0=src, scalar1=0.0)
            else:
                grouped = sb.tile([P, CHUNK, PACK], BF16, name="h_grouped%d" % c, align_bytes=ALIGN)
                nc.scalar.activation(out=grouped[:], in_=src, func=ACT.Relu)
            return grouped[:].rearrange("p v t -> p (v t)")

        h_grouped = [relu(c) for c in range(CHUNKS)]
        h_bytes = CHUNK * PACK * 2
        h0_codes = reused.tile([P, CHUNK], U32, name="h0_codes", align_bytes=ALIGN, offset=h_bytes)

        for c in range(CHUNKS):
            (h_q,) = quantize("h%d" % c, h_grouped[c], codes=h0_codes[:] if c == 0 else None)
            acc = ps.tile([P, CHUNK], F32, name="out_bank%d" % c)
            mx_pass(acc[:], w4_q, h_q, True, True)
            result = sb.tile([P, CHUNK], F32, name="result%d" % c, align_bytes=ALIGN)
            nc.scalar.activation(out=result[:], in_=acc[:], func=ACT.Copy)
            nc.sync.dma_start(out=out[:, c * CHUNK : (c + 1) * CHUNK], in_=result[:])
